import numpy as np
import ml_dtypes


def mxq(x, axis, fmt="e4m3"):
    dtype, down = {"e4m3": (ml_dtypes.float8_e4m3fn, 7), "e5m2": (ml_dtypes.float8_e5m2, 14)}[fmt]
    v = np.moveaxis(np.asarray(x, np.float32).astype(ml_dtypes.bfloat16).astype(np.float64), axis, -1)
    blocks = v.reshape(v.shape[:-1] + (-1, 32))
    amax = np.abs(blocks).max(-1, keepdims=True)
    byte = np.maximum(np.where(amax > 0, np.frexp(amax)[1] - 1 + 127, 0) - down, 1)
    scale = np.exp2(byte - 127.0)
    codes = (blocks / scale).astype(np.float32).astype(dtype).astype(np.float64)
    return np.moveaxis((codes * scale).reshape(v.shape), -1, axis)


WIDE = False


def mx_kscale(k):
    if not WIDE:
        return np.ones(k)
    levels = np.array([10, -10, 5, -5, 0])
    if k % 512:
        return np.exp2(np.random.permutation(np.resize(levels, k // 32))).repeat(32)
    a = np.empty((k // 512, 16))
    for p in range(k // 512):
        a[p, :8] = np.random.permutation(np.resize(levels, 8))
        for g in range(8):
            far = levels[np.abs(levels - a[p, g]) >= 10]
            a[p, g + 8] = far[np.random.randint(len(far))]
    return np.exp2(a.ravel()).repeat(32)


def f64(x):
    return np.asarray(x).astype(np.float64)


def striped(idx):
    return np.tile(idx.reshape(-1, 16).T, (8, 1)).astype(np.uint16)


def unstriped(offs):
    return offs[:16].T.reshape(-1).astype(np.int64)


K, T, S, N = 512, 4096, 1024, 128
P = 2 ** 7


def setup_inputs():
    n = np.random.standard_normal
    s = mx_kscale(K)[:, None]
    return {
        "xT": (n((K, T)) * s).astype(np.float32),
        "tscale": np.tile(np.random.uniform(0.25, 2.0, T), (P, 1)).astype(np.float32),
        "cscale": np.random.uniform(0.5, 1.5, (N, 1)).astype(np.float32),
        "w1": (n((K, N)) / np.sqrt(K) / s).astype(np.float32),
        "offs": striped(np.random.permutation(T)[:S]),
    }


def reference(xT, tscale, cscale, w1, offs):
    xq = mxq(f64(xT)[:, unstriped(offs)], 0, "e4m3")
    y = mxq(f64(w1), 0, "e4m3").T @ xq
    tg = f64(tscale)[:1][:, unstriped(offs)]
    return (f64(cscale) * y) * tg

@@ -1,0 +1,109 @@
+import concourse.mybir as mybir
+from concourse.masks import make_identity
+
+K, T, S, N = 512, 4096, 1024, 128
+FLOPS = 2 * K * S * N
+BYTES = 4 * (K * T + T + N + K * N + N * S) + 2 * 128 * (S // 16)
+
+F32 = mybir.dt.float32
+BF16 = mybir.dt.bfloat16
+U32 = mybir.dt.uint32
+U16 = mybir.dt.uint16
+U8 = mybir.dt.uint8
+FP8X4 = mybir.dt.float8_e4m3fn_x4
+MULT = mybir.AluOpType.mult
+
+P = 128
+PACK = 4
+HALF = S // 2
+PER_PART = T // P
+PER_BANK = 4
+PIECES = ((0, 0, 256), (0, 256, 256), (1, 0, 256), (1, 256, 256))
+
+
+def tile_picked_tokscale_none_l_kernel(tc, xT, tscale, cscale, w1, offs, out):
+    nc = tc.nc
+    with (
+        tc.tile_pool(name="keep", bufs=1) as keep,
+        tc.psum_pool(name="spread", bufs=4) as spread_pool,
+        tc.psum_pool(name="acc", bufs=1) as acc_pool,
+    ):
+        offsets = keep.tile([P, S // 16], U16, name="offsets")
+        ts_rows = keep.tile([P, PER_PART], F32, name="ts_rows")
+        nc.scalar.dma_start(ts_rows[:], tscale[0, :].rearrange("(n m) -> n m", m=PER_PART))
+        x_rows = xT.rearrange("(p t) c -> t p c", t=PACK)
+        planes = [keep.tile([P, T], F32, name=f"plane{t}") for t in range(PACK)]
+        for t in range(PACK):
+            nc.sync.dma_start(planes[t][:], x_rows[t])
+            if t == 0:
+                nc.sync.dma_start(offsets[:], offs)
+        w_raw = keep.tile([P, PACK, N], F32, name="w_raw")
+        nc.sync.dma_start(w_raw[:], w1.rearrange("(p t) n -> p t n", t=PACK))
+        cs = keep.tile([P, 1], F32, name="cs")
+        nc.sync.dma_start(cs[:], cscale)
+
+        ident = keep.tile([P, P], F32, name="ident")
+        make_identity(nc, ident[:])
+        ts_window = keep.tile([P, T], F32, name="ts_window")
+        ts_view = ts_window[:].rearrange("p (n m) -> p n m", m=PER_PART)
+        for b in range(PER_PART // PER_BANK):
+            bank = spread_pool.tile([P, PER_BANK, P], F32, name="bank")
+            for i in range(PER_BANK):
+                m = b * PER_BANK + i
+                nc.tensor.transpose(bank[:, i, :], ts_rows[:, m : m + 1].to_broadcast([P, P]), ident[:])
+            nc.scalar.copy(ts_view[:, :, b * PER_BANK : (b + 1) * PER_BANK], bank[:].rearrange("p i n -> p n i"))
+
+        half_offsets = [offsets[:, h * HALF // 16 : (h + 1) * HALF // 16] for h in range(2)]
+        grouped = [keep.tile([P, HALF, PACK], BF16, name=f"grouped{h}", align_bytes=64) for h in range(2)]
+        low = keep.tile([P, 2, S], F32, name="low")
+        high = keep.tile([P, 2, HALF], F32, name="high")
+        ts_picked = keep.tile([P, S], F32, name="ts_picked")
+
+        nc.vector.tensor_copy(low[:, 0, :], planes[0][:].indirect(offsets[:]))
+        nc.vector.tensor_copy(ts_picked[:], ts_window[:].indirect(offsets[:]))
+        nc.vector.tensor_copy(low[:, 1, :], planes[1][:].indirect(offsets[:]))
+        for h in range(2):
+            nc.scalar.copy(grouped[h][:, :, 0:2], low[:, :, h * HALF : (h + 1) * HALF].rearrange("p t n -> p n t"))
+        for t in (2, 3):
+            nc.vector.tensor_copy(high[:, t - 2, :], planes[t][:].indirect(half_offsets[0]))
+            nc.vector.tensor_copy(grouped[1][:, :, t], planes[t][:].indirect(half_offsets[1]))
+
+        w_grouped = keep.tile([P, N, PACK], BF16, name="w_grouped", align_bytes=64)
+        nc.scalar.copy(w_grouped[:], w_raw[:].rearrange("p t n -> p n t"))
+        for start in (0, 256):
+            cols = slice(start, start + 256)
+            nc.scalar.copy(grouped[0][:, cols, 2:4], high[:, :, cols].rearrange("p t n -> p n t"))
+
+        w_codes = keep.tile([P, N], U32, name="w_codes", align_bytes=64)
+        w_scales = keep.tile([P, N], U8, name="w_scales", align_bytes=64)
+        nc.vector.quantize_mx(
+            out=w_codes[:].bitcast(FP8X4), scales=w_scales[:], in_=w_grouped[:].rearrange("p n t -> p (n t)")
+        )
+
+        accs = []
+        for i, (h, start, width) in enumerate(PIECES):
+            codes = keep.tile([P, width], U32, name=f"codes{i}", align_bytes=64)
+            scales = keep.tile([P, width], U8, name=f"scales{i}", align_bytes=64)
+            nc.vector.quantize_mx(
+                out=codes[:].bitcast(FP8X4),
+                scales=scales[:],
+                in_=grouped[h][:, start : start + width, :].rearrange("p n t -> p (n t)"),
+            )
+            acc = acc_pool.tile([P, width], F32, name=f"acc{i}")
+            nc.tensor.matmul_mx(
+                out=acc[:],
+                lhsT=w_codes[:].bitcast(FP8X4),
+                lhsT_scale=w_scales[:],
+                rhs=codes[:].bitcast(FP8X4),
+                rhs_scale=scales[:],
+                start=True,
+                stop=True,
+            )
+            accs.append(acc)
+
+        for i, (h, start, width) in enumerate(PIECES):
+            cols = slice(h * HALF + start, h * HALF + start + width)
+            result = keep.tile([P, width], F32, name=f"result{i}")
+            nc.vector.scalar_tensor_tensor(result[:], accs[i][:], cs[:, 0:1], ts_picked[:, cols], MULT, MULT)
+            queue = nc.scalar if i % 2 else nc.sync
+            queue.dma_start(out[:, cols], result[:])

@@ -18,15 +18,15 @@ PACK = 4
 HALF = S // 2
 PER_PART = T // P
 PER_BANK = 4
-PIECES = ((0, 0, 256), (0, 256, 256), (1, 0, 256), (1, 256, 256))
+RESULT_AT = (448, 704, 960, 0, 128)
+PIECES = ((0, 0, 256), (0, 256, 256), (1, 0, 256), (1, 256, 128), (1, 384, 128))
 
 
 def tile_picked_tokscale_none_l_kernel(tc, xT, tscale, cscale, w1, offs, out):
     nc = tc.nc
     with (
         tc.tile_pool(name="keep", bufs=1) as keep,
-        tc.psum_pool(name="spread", bufs=4) as spread_pool,
-        tc.psum_pool(name="acc", bufs=1) as acc_pool,
+        tc.psum_pool(name="psum", bufs=1) as psum,
     ):
         offsets = keep.tile([P, S // 16], U16, name="offsets")
         ts_rows = keep.tile([P, PER_PART], F32, name="ts_rows")
@@ -44,35 +44,44 @@ def tile_picked_tokscale_none_l_kernel(tc, xT, tscale, cscale, w1, offs, out):
 
         ident = keep.tile([P, P], F32, name="ident")
         make_identity(nc, ident[:])
-        ts_window = keep.tile([P, T], F32, name="ts_window")
+        ts_window = keep.tile([P, T], F32, name="ts_window", tag="window0")
         ts_view = ts_window[:].rearrange("p (n m) -> p n m", m=PER_PART)
         for b in range(PER_PART // PER_BANK):
-            bank = spread_pool.tile([P, PER_BANK, P], F32, name="bank")
+            bank = psum.tile([P, PER_BANK, P], F32, name=f"spread{b}", tag=f"bank{b}")
             for i in range(PER_BANK):
                 m = b * PER_BANK + i
                 nc.tensor.transpose(bank[:, i, :], ts_rows[:, m : m + 1].to_broadcast([P, P]), ident[:])
             nc.scalar.copy(ts_view[:, :, b * PER_BANK : (b + 1) * PER_BANK], bank[:].rearrange("p i n -> p n i"))
 
         half_offsets = [offsets[:, h * HALF // 16 : (h + 1) * HALF // 16] for h in range(2)]
-        grouped = [keep.tile([P, HALF, PACK], BF16, name=f"grouped{h}", align_bytes=64) for h in range(2)]
         low = keep.tile([P, 2, S], F32, name="low")
-        high = keep.tile([P, 2, HALF], F32, name="high")
         ts_picked = keep.tile([P, S], F32, name="ts_picked")
 
         nc.vector.tensor_copy(low[:, 0, :], planes[0][:].indirect(offsets[:]))
         nc.vector.tensor_copy(ts_picked[:], ts_window[:].indirect(offsets[:]))
         nc.vector.tensor_copy(low[:, 1, :], planes[1][:].indirect(offsets[:]))
+        staging = keep.tile([P, HALF + S], F32, name="staging")
+        pair_words = [keep.tile([P, S], F32, name="pairs0", tag="window0")[:], staging[:, HALF:]]
+        pairs = [words.bitcast(BF16).rearrange("p (u n e) -> p u n e", u=2, e=2) for words in pair_words]
         for h in range(2):
-            nc.scalar.copy(grouped[h][:, :, 0:2], low[:, :, h * HALF : (h + 1) * HALF].rearrange("p t n -> p n t"))
+            nc.scalar.copy(pairs[h][:, 0, :, :], low[:, :, h * HALF : (h + 1) * HALF].rearrange("p t n -> p n t"))
         for t in (2, 3):
-            nc.vector.tensor_copy(high[:, t - 2, :], planes[t][:].indirect(half_offsets[0]))
-            nc.vector.tensor_copy(grouped[1][:, :, t], planes[t][:].indirect(half_offsets[1]))
+            for h in range(2):
+                nc.vector.tensor_copy(pairs[h][:, 1, :, t - 2], planes[t][:].indirect(half_offsets[h]))
 
         w_grouped = keep.tile([P, N, PACK], BF16, name="w_grouped", align_bytes=64)
-        nc.scalar.copy(w_grouped[:], w_raw[:].rearrange("p t n -> p n t"))
-        for start in (0, 256):
-            cols = slice(start, start + 256)
-            nc.scalar.copy(grouped[0][:, cols, 2:4], high[:, :, cols].rearrange("p t n -> p n t"))
+        nc.scalar.copy(
+            w_grouped[:].rearrange("p (c i) t -> p c t i", i=4), w_raw[:].rearrange("p t (c i) -> p c t i", i=4)
+        )
+        grouped = []
+        for i, (h, start, width) in enumerate(PIECES):
+            piece = keep.tile([P, width * PACK], BF16, name=f"grouped{i}", align_bytes=64)
+            words = pair_words[h].bitcast(U32).rearrange("p (u n) -> p u n", u=2)
+            nc.scalar.copy(
+                piece[:].bitcast(U32).rearrange("p (n u) -> p n u", u=2),
+                words[:, :, start : start + width].rearrange("p u n -> p n u"),
+            )
+            grouped.append(piece)
 
         w_codes = keep.tile([P, N], U32, name="w_codes", align_bytes=64)
         w_scales = keep.tile([P, N], U8, name="w_scales", align_bytes=64)
@@ -87,9 +96,9 @@ def tile_picked_tokscale_none_l_kernel(tc, xT, tscale, cscale, w1, offs, out):
             nc.vector.quantize_mx(
                 out=codes[:].bitcast(FP8X4),
                 scales=scales[:],
-                in_=grouped[h][:, start : start + width, :].rearrange("p n t -> p (n t)"),
+                in_=grouped[i][:],
             )
-            acc = acc_pool.tile([P, width], F32, name=f"acc{i}")
+            acc = psum.tile([P, width], F32, name=f"acc{i}", tag=f"bank{i}")
             nc.tensor.matmul_mx(
                 out=acc[:],
                 lhsT=w_codes[:].bitcast(FP8X4),
@@ -103,7 +112,7 @@ def tile_picked_tokscale_none_l_kernel(tc, xT, tscale, cscale, w1, offs, out):
 
         for i, (h, start, width) in enumerate(PIECES):
             cols = slice(h * HALF + start, h * HALF + start + width)
-            result = keep.tile([P, width], F32, name=f"result{i}")
-            nc.vector.scalar_tensor_tensor(result[:], accs[i][:], cs[:, 0:1], ts_picked[:, cols], MULT, MULT)
+            result = staging[:, RESULT_AT[i] : RESULT_AT[i] + width]
+            nc.vector.scalar_tensor_tensor(result, accs[i][:], cs[:, 0:1], ts_picked[:, cols], MULT, MULT)
             queue = nc.scalar if i % 2 else nc.sync
-            queue.dma_start(out[:, cols], result[:])
+            queue.dma_start(out[:, cols], result)

@@ -78,8 +78,8 @@ def tile_picked_tokscale_none_l_kernel(tc, xT, tscale, cscale, w1, offs, out):
             piece = keep.tile([P, width * PACK], BF16, name=f"grouped{i}", align_bytes=64)
             words = pair_words[h].bitcast(U32).rearrange("p (u n) -> p u n", u=2)
             nc.scalar.copy(
-                piece[:].bitcast(U32).rearrange("p (n u) -> p n u", u=2),
-                words[:, :, start : start + width].rearrange("p u n -> p n u"),
+                piece[:].bitcast(U32).rearrange("p (c i u) -> p c u i", i=2, u=2),
+                words[:, :, start : start + width].rearrange("p u (c i) -> p c u i", i=2),
             )
             grouped.append(piece)
 

@@ -12,14 +12,16 @@ U16 = mybir.dt.uint16
 U8 = mybir.dt.uint8
 FP8X4 = mybir.dt.float8_e4m3fn_x4
 MULT = mybir.AluOpType.mult
+ADD = mybir.AluOpType.add
+COPY = mybir.ActivationFunctionType.Copy
 
 P = 128
 PACK = 4
 HALF = S // 2
 PER_PART = T // P
 PER_BANK = 4
-RESULT_AT = (448, 704, 960, 0, 128)
-PIECES = ((0, 0, 256), (0, 256, 256), (1, 0, 256), (1, 256, 128), (1, 384, 128))
+CHUNKS = ((1024, "scalar"), (1024, "scalar"), (1024, "vector"), (768, "vector"), (256, "scalar"))
+PIECES = (256, 256, 256, 128, 128)
 
 
 def tile_picked_tokscale_none_l_kernel(tc, xT, tscale, cscale, w1, offs, out):
@@ -33,10 +35,16 @@ def tile_picked_tokscale_none_l_kernel(tc, xT, tscale, cscale, w1, offs, out):
         nc.scalar.dma_start(ts_rows[:], tscale[0, :].rearrange("(n m) -> n m", m=PER_PART))
         x_rows = xT.rearrange("(p t) c -> t p c", t=PACK)
         planes = [keep.tile([P, T], F32, name=f"plane{t}") for t in range(PACK)]
-        for t in range(PACK):
+        for t in range(PACK - 1):
             nc.sync.dma_start(planes[t][:], x_rows[t])
             if t == 0:
                 nc.sync.dma_start(offsets[:], offs)
+        spans = []
+        at = 0
+        for width, engine in CHUNKS:
+            spans.append((slice(at, at + width), engine))
+            nc.sync.dma_start(planes[3][:, at : at + width], x_rows[3][:, at : at + width])
+            at = at + width
         w_raw = keep.tile([P, PACK, N], F32, name="w_raw")
         nc.sync.dma_start(w_raw[:], w1.rearrange("(p t) n -> p t n", t=PACK))
         cs = keep.tile([P, 1], F32, name="cs")
@@ -44,7 +52,7 @@ def tile_picked_tokscale_none_l_kernel(tc, xT, tscale, cscale, w1, offs, out):
 
         ident = keep.tile([P, P], F32, name="ident")
         make_identity(nc, ident[:])
-        ts_window = keep.tile([P, T], F32, name="ts_window", tag="window0")
+        ts_window = keep.tile([P, T], F32, name="ts_window")
         ts_view = ts_window[:].rearrange("p (n m) -> p n m", m=PER_PART)
         for b in range(PER_PART // PER_BANK):
             bank = psum.tile([P, PER_BANK, P], F32, name=f"spread{b}", tag=f"bank{b}")
@@ -54,50 +62,45 @@ def tile_picked_tokscale_none_l_kernel(tc, xT, tscale, cscale, w1, offs, out):
             nc.scalar.copy(ts_view[:, :, b * PER_BANK : (b + 1) * PER_BANK], bank[:].rearrange("p i n -> p n i"))
 
         half_offsets = [offsets[:, h * HALF // 16 : (h + 1) * HALF // 16] for h in range(2)]
-        low = keep.tile([P, 2, S], F32, name="low")
         ts_picked = keep.tile([P, S], F32, name="ts_picked")
+        grouped = keep.tile([P, S * PACK], BF16, name="grouped", align_bytes=64)
+        slots = grouped[:].rearrange("p (n t) -> p n t", t=PACK)
 
-        nc.vector.tensor_copy(low[:, 0, :], planes[0][:].indirect(offsets[:]))
+        nc.vector.tensor_copy(slots[:, :, 0], planes[0][:].indirect(offsets[:]))
         nc.vector.tensor_copy(ts_picked[:], ts_window[:].indirect(offsets[:]))
-        nc.vector.tensor_copy(low[:, 1, :], planes[1][:].indirect(offsets[:]))
-        staging = keep.tile([P, HALF + S], F32, name="staging")
-        pair_words = [keep.tile([P, S], F32, name="pairs0", tag="window0")[:], staging[:, HALF:]]
-        pairs = [words.bitcast(BF16).rearrange("p (u n e) -> p u n e", u=2, e=2) for words in pair_words]
-        for h in range(2):
-            nc.scalar.copy(pairs[h][:, 0, :, :], low[:, :, h * HALF : (h + 1) * HALF].rearrange("p t n -> p n t"))
-        for t in (2, 3):
-            for h in range(2):
-                nc.vector.tensor_copy(pairs[h][:, 1, :, t - 2], planes[t][:].indirect(half_offsets[h]))
+        nc.vector.tensor_copy(slots[:, :, 1], planes[1][:].indirect(offsets[:]))
+        nc.vector.tensor_copy(slots[:, :, 2], planes[2][:].indirect(offsets[:]))
+
+        last16 = keep.tile([P, T], BF16, name="last16")
+        for cols, engine in spans:
+            if engine == "scalar":
+                nc.scalar.copy(last16[:, cols], planes[3][:, cols])
+            else:
+                nc.vector.tensor_copy(last16[:, cols], planes[3][:, cols])
+        nc.vector.tensor_copy(slots[:, :HALF, 3], planes[3][:].indirect(half_offsets[0]))
+        nc.scalar.activation(slots[:, HALF:, 3], last16[:].indirect(half_offsets[1]), COPY)
 
         w_grouped = keep.tile([P, N, PACK], BF16, name="w_grouped", align_bytes=64)
-        nc.scalar.copy(
+        nc.vector.tensor_copy(
             w_grouped[:].rearrange("p (c i) t -> p c t i", i=4), w_raw[:].rearrange("p t (c i) -> p c t i", i=4)
         )
-        grouped = []
-        for i, (h, start, width) in enumerate(PIECES):
-            piece = keep.tile([P, width * PACK], BF16, name=f"grouped{i}", align_bytes=64)
-            words = pair_words[h].bitcast(U32).rearrange("p (u n) -> p u n", u=2)
-            nc.scalar.copy(
-                piece[:].bitcast(U32).rearrange("p (c i u) -> p c u i", i=2, u=2),
-                words[:, :, start : start + width].rearrange("p u (c i) -> p c u i", i=2),
-            )
-            grouped.append(piece)
-
         w_codes = keep.tile([P, N], U32, name="w_codes", align_bytes=64)
         w_scales = keep.tile([P, N], U8, name="w_scales", align_bytes=64)
-        nc.vector.quantize_mx(
-            out=w_codes[:].bitcast(FP8X4), scales=w_scales[:], in_=w_grouped[:].rearrange("p n t -> p (n t)")
-        )
 
         accs = []
-        for i, (h, start, width) in enumerate(PIECES):
+        at = 0
+        for i, width in enumerate(PIECES):
             codes = keep.tile([P, width], U32, name=f"codes{i}", align_bytes=64)
             scales = keep.tile([P, width], U8, name=f"scales{i}", align_bytes=64)
             nc.vector.quantize_mx(
                 out=codes[:].bitcast(FP8X4),
                 scales=scales[:],
-                in_=grouped[i][:],
+                in_=grouped[:, at * PACK : (at + width) * PACK],
             )
+            if i == 0:
+                nc.vector.quantize_mx(
+                    out=w_codes[:].bitcast(FP8X4), scales=w_scales[:], in_=w_grouped[:].rearrange("p n t -> p (n t)")
+                )
             acc = psum.tile([P, width], F32, name=f"acc{i}", tag=f"bank{i}")
             nc.tensor.matmul_mx(
                 out=acc[:],
@@ -108,11 +111,11 @@ def tile_picked_tokscale_none_l_kernel(tc, xT, tscale, cscale, w1, offs, out):
                 start=True,
                 stop=True,
             )
-            accs.append(acc)
+            accs.append((acc, slice(at, at + width)))
+            at = at + width
 
-        for i, (h, start, width) in enumerate(PIECES):
-            cols = slice(h * HALF + start, h * HALF + start + width)
-            result = staging[:, RESULT_AT[i] : RESULT_AT[i] + width]
-            nc.vector.scalar_tensor_tensor(result, accs[i][:], cs[:, 0:1], ts_picked[:, cols], MULT, MULT)
+        result = keep.tile([P, S], F32, name="result")
+        for i, (acc, cols) in enumerate(accs):
+            nc.vector.scalar_tensor_tensor(result[:, cols], acc[:], cs[:, 0:1], ts_picked[:, cols], MULT, MULT)
             queue = nc.scalar if i % 2 else nc.sync
-            queue.dma_start(out[:, cols], result)
+            queue.dma_start(out[:, cols], result[:, cols])

@@ -20,7 +20,7 @@ PACK = 4
 HALF = S // 2
 PER_PART = T // P
 PER_BANK = 4
-CHUNKS = ((1024, "scalar"), (1024, "scalar"), (1024, "vector"), (768, "vector"), (256, "scalar"))
+CHUNKS = ((1280, "scalar"), (1280, "scalar"), (1024, "vector"), (512, "scalar"))
 PIECES = (256, 256, 256, 128, 128)
 
 
@@ -66,10 +66,15 @@ def tile_picked_tokscale_none_l_kernel(tc, xT, tscale, cscale, w1, offs, out):
         grouped = keep.tile([P, S * PACK], BF16, name="grouped", align_bytes=64)
         slots = grouped[:].rearrange("p (n t) -> p n t", t=PACK)
 
-        nc.vector.tensor_copy(slots[:, :, 0], planes[0][:].indirect(offsets[:]))
+        low = keep.tile([P, 2, S], F32, name="low")
+        nc.vector.tensor_copy(low[:, 0, :], planes[0][:].indirect(offsets[:]))
         nc.vector.tensor_copy(ts_picked[:], ts_window[:].indirect(offsets[:]))
-        nc.vector.tensor_copy(slots[:, :, 1], planes[1][:].indirect(offsets[:]))
-        nc.vector.tensor_copy(slots[:, :, 2], planes[2][:].indirect(offsets[:]))
+        for h in range(2):
+            cols = slice(h * HALF, (h + 1) * HALF)
+            nc.vector.tensor_copy(low[:, 1, cols], planes[1][:].indirect(half_offsets[h]))
+            nc.scalar.copy(slots[:, cols, 0:2], low[:, :, cols].rearrange("p t n -> p n t"))
+        for h in range(2):
+            nc.vector.tensor_copy(slots[:, h * HALF : (h + 1) * HALF, 2], planes[2][:].indirect(half_offsets[h]))
 
         last16 = keep.tile([P, T], BF16, name="last16")
         for cols, engine in spans:

@@ -86,9 +86,7 @@ def tile_picked_tokscale_none_l_kernel(tc, xT, tscale, cscale, w1, offs, out):
         nc.scalar.activation(slots[:, HALF:, 3], last16[:].indirect(half_offsets[1]), COPY)
 
         w_grouped = keep.tile([P, N, PACK], BF16, name="w_grouped", align_bytes=64)
-        nc.vector.tensor_copy(
-            w_grouped[:].rearrange("p (c i) t -> p c t i", i=4), w_raw[:].rearrange("p t (c i) -> p c t i", i=4)
-        )
+        nc.gpsimd.tensor_scalar(w_grouped[:], w_raw[:].rearrange("p t n -> p n t"), 1.0, 0.0, MULT, ADD)
         w_codes = keep.tile([P, N], U32, name="w_codes", align_bytes=64)
         w_scales = keep.tile([P, N], U8, name="w_scales", align_bytes=64)
 

@@ -20,7 +20,7 @@ PACK = 4
 HALF = S // 2
 PER_PART = T // P
 PER_BANK = 4
-CHUNKS = ((1280, "scalar"), (1280, "scalar"), (1024, "vector"), (512, "scalar"))
+CHUNKS = ((("gpsimd", 1024), ("scalar", 1536)), (("vector", 512), ("scalar", 512)), (("gpsimd", 512),))
 PIECES = (256, 256, 256, 128, 128)
 
 
@@ -41,10 +41,12 @@ def tile_picked_tokscale_none_l_kernel(tc, xT, tscale, cscale, w1, offs, out):
                 nc.sync.dma_start(offsets[:], offs)
         spans = []
         at = 0
-        for width, engine in CHUNKS:
-            spans.append((slice(at, at + width), engine))
-            nc.sync.dma_start(planes[3][:, at : at + width], x_rows[3][:, at : at + width])
-            at = at + width
+        for shares in CHUNKS:
+            begin = at
+            for engine, width in shares:
+                spans.append((engine, slice(at, at + width)))
+                at = at + width
+            nc.sync.dma_start(planes[3][:, begin:at], x_rows[3][:, begin:at])
         w_raw = keep.tile([P, PACK, N], F32, name="w_raw")
         nc.sync.dma_start(w_raw[:], w1.rearrange("(p t) n -> p t n", t=PACK))
         cs = keep.tile([P, 1], F32, name="cs")
@@ -77,11 +79,13 @@ def tile_picked_tokscale_none_l_kernel(tc, xT, tscale, cscale, w1, offs, out):
             nc.vector.tensor_copy(slots[:, h * HALF : (h + 1) * HALF, 2], planes[2][:].indirect(half_offsets[h]))
 
         last16 = keep.tile([P, T], BF16, name="last16")
-        for cols, engine in spans:
+        for engine, cols in spans:
             if engine == "scalar":
                 nc.scalar.copy(last16[:, cols], planes[3][:, cols])
-            else:
+            elif engine == "vector":
                 nc.vector.tensor_copy(last16[:, cols], planes[3][:, cols])
+            else:
+                nc.gpsimd.tensor_scalar(last16[:, cols], planes[3][:, cols], 1.0, 0.0, MULT, ADD)
         nc.vector.tensor_copy(slots[:, :HALF, 3], planes[3][:].indirect(half_offsets[0]))
         nc.scalar.activation(slots[:, HALF:, 3], last16[:].indirect(half_offsets[1]), COPY)
 

@@ -20,7 +20,7 @@ PACK = 4
 HALF = S // 2
 PER_PART = T // P
 PER_BANK = 4
-CHUNKS = ((("gpsimd", 1024), ("scalar", 1536)), (("vector", 512), ("scalar", 512)), (("gpsimd", 512),))
+CHUNKS = ((("vector", 1024), ("scalar", 1280)), (("vector", 768), ("scalar", 512)), (("gpsimd", 256), ("scalar", 256)))
 PIECES = (256, 256, 256, 128, 128)
 
 
@@ -32,7 +32,7 @@ def tile_picked_tokscale_none_l_kernel(tc, xT, tscale, cscale, w1, offs, out):
     ):
         offsets = keep.tile([P, S // 16], U16, name="offsets")
         ts_rows = keep.tile([P, PER_PART], F32, name="ts_rows")
-        nc.scalar.dma_start(ts_rows[:], tscale[0, :].rearrange("(n m) -> n m", m=PER_PART))
+        nc.sync.dma_start(ts_rows[:], tscale[0, :].rearrange("(n m) -> n m", m=PER_PART))
         x_rows = xT.rearrange("(p t) c -> t p c", t=PACK)
         planes = [keep.tile([P, T], F32, name=f"plane{t}") for t in range(PACK)]
         for t in range(PACK - 1):
@@ -75,8 +75,10 @@ def tile_picked_tokscale_none_l_kernel(tc, xT, tscale, cscale, w1, offs, out):
             cols = slice(h * HALF, (h + 1) * HALF)
             nc.vector.tensor_copy(low[:, 1, cols], planes[1][:].indirect(half_offsets[h]))
             nc.scalar.copy(slots[:, cols, 0:2], low[:, :, cols].rearrange("p t n -> p n t"))
-        for h in range(2):
-            nc.vector.tensor_copy(slots[:, h * HALF : (h + 1) * HALF, 2], planes[2][:].indirect(half_offsets[h]))
+        third = keep.tile([P, HALF], BF16, name="third")
+        nc.vector.tensor_copy(third[:], planes[2][:].indirect(half_offsets[1]))
+        nc.vector.tensor_copy(slots[:, :HALF, 2], planes[2][:].indirect(half_offsets[0]))
+        nc.gpsimd.tensor_scalar(slots[:, HALF:, 2], third[:], 1.0, 0.0, MULT, ADD)
 
         last16 = keep.tile([P, T], BF16, name="last16")
         for engine, cols in spans:

@@ -21,7 +21,7 @@ HALF = S // 2
 PER_PART = T // P
 PER_BANK = 4
 CHUNKS = ((("vector", 1024), ("scalar", 1280)), (("vector", 768), ("scalar", 512)), (("gpsimd", 256), ("scalar", 256)))
-PIECES = (256, 256, 256, 128, 128)
+PIECES = (256, 256, 256, 256)
 
 
 def tile_picked_tokscale_none_l_kernel(tc, xT, tscale, cscale, w1, offs, out):
@@ -47,7 +47,7 @@ def tile_picked_tokscale_none_l_kernel(tc, xT, tscale, cscale, w1, offs, out):
                 spans.append((engine, slice(at, at + width)))
                 at = at + width
             nc.sync.dma_start(planes[3][:, begin:at], x_rows[3][:, begin:at])
-        w_raw = keep.tile([P, PACK, N], F32, name="w_raw")
+        w_raw = keep.tile([P, PACK, N], F32, name="w_raw", tag="shared", align_bytes=64)
         nc.sync.dma_start(w_raw[:], w1.rearrange("(p t) n -> p t n", t=PACK))
         cs = keep.tile([P, 1], F32, name="cs")
         nc.sync.dma_start(cs[:], cscale)
@@ -96,26 +96,26 @@ def tile_picked_tokscale_none_l_kernel(tc, xT, tscale, cscale, w1, offs, out):
         w_codes = keep.tile([P, N], U32, name="w_codes", align_bytes=64)
         w_scales = keep.tile([P, N], U8, name="w_scales", align_bytes=64)
 
+        nc.vector.quantize_mx(
+            out=w_codes[:].bitcast(FP8X4), scales=w_scales[:], in_=w_grouped[:].rearrange("p n t -> p (n t)")
+        )
+        all_codes = keep.tile([P, S], U32, name="all_codes", tag="shared", align_bytes=64)
         accs = []
         at = 0
         for i, width in enumerate(PIECES):
-            codes = keep.tile([P, width], U32, name=f"codes{i}", align_bytes=64)
+            codes = all_codes[:, at : at + width]
             scales = keep.tile([P, width], U8, name=f"scales{i}", align_bytes=64)
             nc.vector.quantize_mx(
-                out=codes[:].bitcast(FP8X4),
+                out=codes.bitcast(FP8X4),
                 scales=scales[:],
                 in_=grouped[:, at * PACK : (at + width) * PACK],
             )
-            if i == 0:
-                nc.vector.quantize_mx(
-                    out=w_codes[:].bitcast(FP8X4), scales=w_scales[:], in_=w_grouped[:].rearrange("p n t -> p (n t)")
-                )
             acc = psum.tile([P, width], F32, name=f"acc{i}", tag=f"bank{i}")
             nc.tensor.matmul_mx(
                 out=acc[:],
                 lhsT=w_codes[:].bitcast(FP8X4),
                 lhsT_scale=w_scales[:],
-                rhs=codes[:].bitcast(FP8X4),
+                rhs=codes.bitcast(FP8X4),
                 rhs_scale=scales[:],
                 start=True,
                 stop=True,
@@ -126,5 +126,5 @@ def tile_picked_tokscale_none_l_kernel(tc, xT, tscale, cscale, w1, offs, out):
         result = keep.tile([P, S], F32, name="result")
         for i, (acc, cols) in enumerate(accs):
             nc.vector.scalar_tensor_tensor(result[:, cols], acc[:], cs[:, 0:1], ts_picked[:, cols], MULT, MULT)
-            queue = nc.scalar if i % 2 else nc.sync
+            queue = nc.sync if i % 2 else nc.scalar
             queue.dma_start(out[:, cols], result[:, cols])

@@ -124,7 +124,6 @@ def tile_picked_tokscale_none_l_kernel(tc, xT, tscale, cscale, w1, offs, out):
             at = at + width
 
         result = keep.tile([P, S], F32, name="result")
-        for i, (acc, cols) in enumerate(accs):
+        for acc, cols in accs:
             nc.vector.scalar_tensor_tensor(result[:, cols], acc[:], cs[:, 0:1], ts_picked[:, cols], MULT, MULT)
-            queue = nc.sync if i % 2 else nc.scalar
-            queue.dma_start(out[:, cols], result[:, cols])
+            nc.sync.dma_start(out[:, cols], result[:, cols])

@@ -20,7 +20,7 @@ PACK = 4
 HALF = S // 2
 PER_PART = T // P
 PER_BANK = 4
-CHUNKS = ((("vector", 1024), ("scalar", 1280)), (("vector", 768), ("scalar", 512)), (("gpsimd", 256), ("scalar", 256)))
+CHUNKS = ((("vector", 896), ("scalar", 1408)), (("vector", 768), ("scalar", 512)), (("gpsimd", 256), ("scalar", 256)))
 PIECES = (256, 256, 256, 256)
 
 
@@ -32,7 +32,7 @@ def tile_picked_tokscale_none_l_kernel(tc, xT, tscale, cscale, w1, offs, out):
     ):
         offsets = keep.tile([P, S // 16], U16, name="offsets")
         ts_rows = keep.tile([P, PER_PART], F32, name="ts_rows")
-        nc.sync.dma_start(ts_rows[:], tscale[0, :].rearrange("(n m) -> n m", m=PER_PART))
+        nc.scalar.dma_start(ts_rows[:], tscale[0, :].rearrange("(n m) -> n m", m=PER_PART))
         x_rows = xT.rearrange("(p t) c -> t p c", t=PACK)
         planes = [keep.tile([P, T], F32, name=f"plane{t}") for t in range(PACK)]
         for t in range(PACK - 1):

@@ -124,6 +124,12 @@ def tile_picked_tokscale_none_l_kernel(tc, xT, tscale, cscale, w1, offs, out):
             at = at + width
 
         result = keep.tile([P, S], F32, name="result")
-        for acc, cols in accs:
-            nc.vector.scalar_tensor_tensor(result[:, cols], acc[:], cs[:, 0:1], ts_picked[:, cols], MULT, MULT)
-            nc.sync.dma_start(out[:, cols], result[:, cols])
+        for i, (acc, cols) in enumerate(accs):
+            parts = 2 if i == len(accs) - 1 else 1
+            width = (cols.stop - cols.start) // parts
+            for part in range(parts):
+                here = slice(cols.start + part * width, cols.start + (part + 1) * width)
+                nc.vector.scalar_tensor_tensor(
+                    result[:, here], acc[:, part * width : (part + 1) * width], cs[:, 0:1], ts_picked[:, here], MULT, MULT
+                )
+                nc.sync.dma_start(out[:, here], result[:, here])

@@ -110,26 +110,36 @@ def tile_picked_tokscale_none_l_kernel(tc, xT, tscale, cscale, w1, offs, out):
                 scales=scales[:],
                 in_=grouped[:, at * PACK : (at + width) * PACK],
             )
-            acc = psum.tile([P, width], F32, name=f"acc{i}", tag=f"bank{i}")
-            nc.tensor.matmul_mx(
-                out=acc[:],
-                lhsT=w_codes[:].bitcast(FP8X4),
-                lhsT_scale=w_scales[:],
-                rhs=codes.bitcast(FP8X4),
-                rhs_scale=scales[:],
-                start=True,
-                stop=True,
-            )
-            accs.append((acc, slice(at, at + width)))
+            parts = 2 if i == 0 else 1
+            step = width // parts
+            for part in range(parts):
+                sub = slice(part * step, (part + 1) * step)
+                acc = psum.tile([P, step], F32, name=f"acc{len(accs)}", tag=f"bank{len(accs)}")
+                nc.tensor.matmul_mx(
+                    out=acc[:],
+                    lhsT=w_codes[:].bitcast(FP8X4),
+                    lhsT_scale=w_scales[:],
+                    rhs=codes[:, sub].bitcast(FP8X4),
+                    rhs_scale=scales[:, sub],
+                    start=True,
+                    stop=True,
+                )
+                accs.append((acc, slice(at + sub.start, at + sub.stop)))
             at = at + width
 
         result = keep.tile([P, S], F32, name="result")
         for i, (acc, cols) in enumerate(accs):
+            if i == 1:
+                aside = keep.tile([P, cols.stop - cols.start], F32, name="aside")
+                nc.scalar.activation(aside[:], acc[:], COPY, scale=cs[:, 0:1])
+                nc.gpsimd.tensor_tensor(result[:, cols], aside[:], ts_picked[:, cols], MULT)
+                nc.scalar.dma_start(out[:, cols], result[:, cols])
+                continue
             parts = 2 if i == len(accs) - 1 else 1
             width = (cols.stop - cols.start) // parts
             for part in range(parts):
                 here = slice(cols.start + part * width, cols.start + (part + 1) * width)
                 nc.vector.scalar_tensor_tensor(
-                    result[:, here], acc[:, part * width : (part + 1) * width], cs[:, 0:1], ts_picked[:, here], MULT, MULT
+                    result[:, here], ts_picked[:, here], cs[:, 0:1], acc[:, part * width : (part + 1) * width], MULT, MULT
                 )
                 nc.sync.dma_start(out[:, here], result[:, here])

@@ -21,7 +21,11 @@ HALF = S // 2
 PER_PART = T // P
 PER_BANK = 4
 CHUNKS = ((("vector", 896), ("scalar", 1408)), (("vector", 768), ("scalar", 512)), (("gpsimd", 256), ("scalar", 256)))
-PIECES = (256, 256, 256, 256)
+QUANT = 256
+PART = 128
+QUANT_ORDER = (1, 0, 2, 3)
+ASIDE = 3
+STORES = ((2, 2), (0, 0), (1, 1), (3, 5), (6, 7))
 
 
 def tile_picked_tokscale_none_l_kernel(tc, xT, tscale, cscale, w1, offs, out):
@@ -101,20 +105,18 @@ def tile_picked_tokscale_none_l_kernel(tc, xT, tscale, cscale, w1, offs, out):
         )
         all_codes = keep.tile([P, S], U32, name="all_codes", tag="shared", align_bytes=64)
         accs = []
-        at = 0
-        for i, width in enumerate(PIECES):
-            codes = all_codes[:, at : at + width]
-            scales = keep.tile([P, width], U8, name=f"scales{i}", align_bytes=64)
+        for i in QUANT_ORDER:
+            at = i * QUANT
+            codes = all_codes[:, at : at + QUANT]
+            scales = keep.tile([P, QUANT], U8, name=f"scales{i}", align_bytes=64)
             nc.vector.quantize_mx(
                 out=codes.bitcast(FP8X4),
                 scales=scales[:],
-                in_=grouped[:, at * PACK : (at + width) * PACK],
+                in_=grouped[:, at * PACK : (at + QUANT) * PACK],
             )
-            parts = 2 if i == 0 else 1
-            step = width // parts
-            for part in range(parts):
-                sub = slice(part * step, (part + 1) * step)
-                acc = psum.tile([P, step], F32, name=f"acc{len(accs)}", tag=f"bank{len(accs)}")
+            for part in range(QUANT // PART):
+                sub = slice(part * PART, (part + 1) * PART)
+                acc = psum.tile([P, PART], F32, name=f"acc{len(accs)}", tag=f"bank{len(accs)}")
                 nc.tensor.matmul_mx(
                     out=acc[:],
                     lhsT=w_codes[:].bitcast(FP8X4),
@@ -124,22 +126,21 @@ def tile_picked_tokscale_none_l_kernel(tc, xT, tscale, cscale, w1, offs, out):
                     start=True,
                     stop=True,
                 )
-                accs.append((acc, slice(at + sub.start, at + sub.stop)))
-            at = at + width
+                accs.append((acc, at // PART + part))
 
         result = keep.tile([P, S], F32, name="result")
-        for i, (acc, cols) in enumerate(accs):
-            if i == 1:
-                aside = keep.tile([P, cols.stop - cols.start], F32, name="aside")
+        done = set()
+        for acc, part in accs:
+            cols = slice(part * PART, (part + 1) * PART)
+            if part == ASIDE:
+                aside = keep.tile([P, PART], F32, name="aside")
                 nc.scalar.activation(aside[:], acc[:], COPY, scale=cs[:, 0:1])
                 nc.gpsimd.tensor_tensor(result[:, cols], aside[:], ts_picked[:, cols], MULT)
-                nc.scalar.dma_start(out[:, cols], result[:, cols])
-                continue
-            parts = 2 if i == len(accs) - 1 else 1
-            width = (cols.stop - cols.start) // parts
-            for part in range(parts):
-                here = slice(cols.start + part * width, cols.start + (part + 1) * width)
-                nc.vector.scalar_tensor_tensor(
-                    result[:, here], ts_picked[:, here], cs[:, 0:1], acc[:, part * width : (part + 1) * width], MULT, MULT
-                )
-                nc.sync.dma_start(out[:, here], result[:, here])
+            else:
+                nc.vector.scalar_tensor_tensor(result[:, cols], ts_picked[:, cols], cs[:, 0:1], acc[:], MULT, MULT)
+            done.add(part)
+            for first, last in STORES:
+                if first <= part <= last and all(q in done for q in range(first, last + 1)):
+                    run = slice(first * PART, (last + 1) * PART)
+                    queue = nc.scalar if first <= ASIDE <= last else nc.sync
+                    queue.dma_start(out[:, run], result[:, run])

@@ -20,7 +20,7 @@ PACK = 4
 HALF = S // 2
 PER_PART = T // P
 PER_BANK = 4
-CHUNKS = ((("vector", 896), ("scalar", 1408)), (("vector", 768), ("scalar", 512)), (("gpsimd", 256), ("scalar", 256)))
+PIECES = (("gpsimd", 512, 640), ("scalar", 640, 768), ("scalar", 768, 1024))
 QUANT = 256
 PART = 128
 QUANT_ORDER = (1, 0, 2, 3)
@@ -39,18 +39,10 @@ def tile_picked_tokscale_none_l_kernel(tc, xT, tscale, cscale, w1, offs, out):
         nc.scalar.dma_start(ts_rows[:], tscale[0, :].rearrange("(n m) -> n m", m=PER_PART))
         x_rows = xT.rearrange("(p t) c -> t p c", t=PACK)
         planes = [keep.tile([P, T], F32, name=f"plane{t}") for t in range(PACK)]
-        for t in range(PACK - 1):
+        for t in range(PACK):
             nc.sync.dma_start(planes[t][:], x_rows[t])
             if t == 0:
                 nc.sync.dma_start(offsets[:], offs)
-        spans = []
-        at = 0
-        for shares in CHUNKS:
-            begin = at
-            for engine, width in shares:
-                spans.append((engine, slice(at, at + width)))
-                at = at + width
-            nc.sync.dma_start(planes[3][:, begin:at], x_rows[3][:, begin:at])
         w_raw = keep.tile([P, PACK, N], F32, name="w_raw", tag="shared", align_bytes=64)
         nc.sync.dma_start(w_raw[:], w1.rearrange("(p t) n -> p t n", t=PACK))
         cs = keep.tile([P, 1], F32, name="cs")
@@ -65,35 +57,31 @@ def tile_picked_tokscale_none_l_kernel(tc, xT, tscale, cscale, w1, offs, out):
             for i in range(PER_BANK):
                 m = b * PER_BANK + i
                 nc.tensor.transpose(bank[:, i, :], ts_rows[:, m : m + 1].to_broadcast([P, P]), ident[:])
-            nc.scalar.copy(ts_view[:, :, b * PER_BANK : (b + 1) * PER_BANK], bank[:].rearrange("p i n -> p n i"))
+            spread = ts_view[:, :, b * PER_BANK : (b + 1) * PER_BANK]
+            if b % 2 == 0:
+                nc.vector.tensor_copy(spread, bank[:].rearrange("p i n -> p n i"))
+            else:
+                nc.scalar.copy(spread, bank[:].rearrange("p i n -> p n i"))
 
-        half_offsets = [offsets[:, h * HALF // 16 : (h + 1) * HALF // 16] for h in range(2)]
         ts_picked = keep.tile([P, S], F32, name="ts_picked")
         grouped = keep.tile([P, S * PACK], BF16, name="grouped", align_bytes=64)
         slots = grouped[:].rearrange("p (n t) -> p n t", t=PACK)
 
-        low = keep.tile([P, 2, S], F32, name="low")
-        nc.vector.tensor_copy(low[:, 0, :], planes[0][:].indirect(offsets[:]))
-        nc.vector.tensor_copy(ts_picked[:], ts_window[:].indirect(offsets[:]))
-        for h in range(2):
-            cols = slice(h * HALF, (h + 1) * HALF)
-            nc.vector.tensor_copy(low[:, 1, cols], planes[1][:].indirect(half_offsets[h]))
-            nc.scalar.copy(slots[:, cols, 0:2], low[:, :, cols].rearrange("p t n -> p n t"))
-        third = keep.tile([P, HALF], BF16, name="third")
-        nc.vector.tensor_copy(third[:], planes[2][:].indirect(half_offsets[1]))
-        nc.vector.tensor_copy(slots[:, :HALF, 2], planes[2][:].indirect(half_offsets[0]))
-        nc.gpsimd.tensor_scalar(slots[:, HALF:, 2], third[:], 1.0, 0.0, MULT, ADD)
-
-        last16 = keep.tile([P, T], BF16, name="last16")
-        for engine, cols in spans:
-            if engine == "scalar":
-                nc.scalar.copy(last16[:, cols], planes[3][:, cols])
-            elif engine == "vector":
-                nc.vector.tensor_copy(last16[:, cols], planes[3][:, cols])
-            else:
-                nc.gpsimd.tensor_scalar(last16[:, cols], planes[3][:, cols], 1.0, 0.0, MULT, ADD)
-        nc.vector.tensor_copy(slots[:, :HALF, 3], planes[3][:].indirect(half_offsets[0]))
-        nc.scalar.activation(slots[:, HALF:, 3], last16[:].indirect(half_offsets[1]), COPY)
+        for t in range(PACK):
+            nc.vector.tensor_copy(slots[:, :HALF, t], planes[t][:].indirect(offsets[:, : HALF // 16]))
+            if t == 0:
+                nc.vector.tensor_copy(ts_picked[:], ts_window[:].indirect(offsets[:]))
+            staged = []
+            pieces = PIECES if t >= 2 else (("gpsimd", HALF, S),)
+            for engine, a, b in pieces:
+                piece = keep.tile([P, b - a], BF16, name=f"piece{t}_{a}")
+                nc.scalar.activation(piece[:], planes[t][:].indirect(offsets[:, a // 16 : b // 16]), COPY)
+                staged.append(piece)
+            for piece, (engine, a, b) in zip(staged, pieces):
+                if engine == "gpsimd":
+                    nc.gpsimd.tensor_scalar(slots[:, a:b, t], piece[:], 1.0, 0.0, MULT, ADD)
+                else:
+                    nc.scalar.copy(slots[:, a:b, t], piece[:])
 
         w_grouped = keep.tile([P, N, PACK], BF16, name="w_grouped", align_bytes=64)
         nc.gpsimd.tensor_scalar(w_grouped[:], w_raw[:].rearrange("p t n -> p n t"), 1.0, 0.0, MULT, ADD)

@@ -20,7 +20,7 @@ PACK = 4
 HALF = S // 2
 PER_PART = T // P
 PER_BANK = 4
-PIECES = (("gpsimd", 512, 640), ("scalar", 640, 768), ("scalar", 768, 1024))
+PIECES = (("gpsimd", 512, 576), ("scalar", 576, 768), ("scalar", 768, 1024))
 QUANT = 256
 PART = 128
 QUANT_ORDER = (1, 0, 2, 3)
@@ -74,7 +74,7 @@ def tile_picked_tokscale_none_l_kernel(tc, xT, tscale, cscale, w1, offs, out):
             staged = []
             pieces = PIECES if t >= 2 else (("gpsimd", HALF, S),)
             for engine, a, b in pieces:
-                piece = keep.tile([P, b - a], BF16, name=f"piece{t}_{a}")
+                piece = keep.tile([P, b - a], F32 if b - a < PART else BF16, name=f"piece{t}_{a}")
                 nc.scalar.activation(piece[:], planes[t][:].indirect(offsets[:, a // 16 : b // 16]), COPY)
                 staged.append(piece)
             for piece, (engine, a, b) in zip(staged, pieces):

@@ -21,9 +21,9 @@ HALF = S // 2
 PER_PART = T // P
 PER_BANK = 4
 PIECES = (("gpsimd", 512, 576), ("scalar", 576, 768), ("scalar", 768, 1024))
-QUANT = 256
+PLACE = 128
 PART = 128
-QUANT_ORDER = (1, 0, 2, 3)
+QUANTS = ((256, 256), (0, 256), (512, 256), (768, 128), (896, 128))
 ASIDE = 3
 STORES = ((2, 2), (0, 0), (1, 1), (3, 5), (6, 7))
 
@@ -80,6 +80,9 @@ def tile_picked_tokscale_none_l_kernel(tc, xT, tscale, cscale, w1, offs, out):
             for piece, (engine, a, b) in zip(staged, pieces):
                 if engine == "gpsimd":
                     nc.gpsimd.tensor_scalar(slots[:, a:b, t], piece[:], 1.0, 0.0, MULT, ADD)
+                elif t == PACK - 1 and b == S:
+                    for c in range(a, b, PLACE):
+                        nc.scalar.copy(slots[:, c : c + PLACE, t], piece[:, c - a : c - a + PLACE])
                 else:
                     nc.scalar.copy(slots[:, a:b, t], piece[:])
 
@@ -93,16 +96,15 @@ def tile_picked_tokscale_none_l_kernel(tc, xT, tscale, cscale, w1, offs, out):
         )
         all_codes = keep.tile([P, S], U32, name="all_codes", tag="shared", align_bytes=64)
         accs = []
-        for i in QUANT_ORDER:
-            at = i * QUANT
-            codes = all_codes[:, at : at + QUANT]
-            scales = keep.tile([P, QUANT], U8, name=f"scales{i}", align_bytes=64)
+        for at, width in QUANTS:
+            codes = all_codes[:, at : at + width]
+            scales = keep.tile([P, width], U8, name=f"scales{at}", align_bytes=64)
             nc.vector.quantize_mx(
                 out=codes.bitcast(FP8X4),
                 scales=scales[:],
-                in_=grouped[:, at * PACK : (at + QUANT) * PACK],
+                in_=grouped[:, at * PACK : (at + width) * PACK],
             )
-            for part in range(QUANT // PART):
+            for part in range(width // PART):
                 sub = slice(part * PART, (part + 1) * PART)
                 acc = psum.tile([P, PART], F32, name=f"acc{len(accs)}", tag=f"bank{len(accs)}")
                 nc.tensor.matmul_mx(

@@ -17,15 +17,16 @@ COPY = mybir.ActivationFunctionType.Copy
 
 P = 128
 PACK = 4
-HALF = S // 2
 PER_PART = T // P
 PER_BANK = 4
-PIECES = (("gpsimd", 512, 576), ("scalar", 576, 768), ("scalar", 768, 1024))
-PLACE = 128
 PART = 128
-QUANTS = ((256, 256), (0, 256), (512, 256), (768, 128), (896, 128))
-ASIDE = 3
-STORES = ((2, 2), (0, 0), (1, 1), (3, 5), (6, 7))
+ON_VECTOR = (384, 896)
+EARLY_RUNS = ((0, 384), (896, 1024))
+LATE_ON_GPSIMD = (128, 192)
+LATE_ON_SCALAR = ((192, 384), (0, 128), (896, 1024))
+QUANTS = ((640, 256), (384, 256), (128, 256), (0, 128), (896, 128))
+ASIDE = 6
+STORES = ((5, 5), (4, 4), (2, 3), (0, 1), (6, 7))
 
 
 def tile_picked_tokscale_none_l_kernel(tc, xT, tscale, cscale, w1, offs, out):
@@ -67,23 +68,30 @@ def tile_picked_tokscale_none_l_kernel(tc, xT, tscale, cscale, w1, offs, out):
         grouped = keep.tile([P, S * PACK], BF16, name="grouped", align_bytes=64)
         slots = grouped[:].rearrange("p (n t) -> p n t", t=PACK)
 
+        def looked_up(window, a, b):
+            return window[:].indirect(offsets[:, a // 16 : b // 16])
+
+        def gather_on_scalar(t, a, b, dtype):
+            piece = keep.tile([P, b - a], dtype, name=f"piece{t}_{a}")
+            nc.scalar.activation(piece[:], looked_up(planes[t], a, b), COPY)
+            return piece
+
+        def place_on_gpsimd(t, a, b, piece):
+            nc.gpsimd.tensor_scalar(slots[:, a:b, t], piece[:], 1.0, 0.0, MULT, ADD)
+
         for t in range(PACK):
-            nc.vector.tensor_copy(slots[:, :HALF, t], planes[t][:].indirect(offsets[:, : HALF // 16]))
+            a, b = ON_VECTOR
+            nc.vector.tensor_copy(slots[:, a:b, t], looked_up(planes[t], a, b))
             if t == 0:
-                nc.vector.tensor_copy(ts_picked[:], ts_window[:].indirect(offsets[:]))
-            staged = []
-            pieces = PIECES if t >= 2 else (("gpsimd", HALF, S),)
-            for engine, a, b in pieces:
-                piece = keep.tile([P, b - a], F32 if b - a < PART else BF16, name=f"piece{t}_{a}")
-                nc.scalar.activation(piece[:], planes[t][:].indirect(offsets[:, a // 16 : b // 16]), COPY)
-                staged.append(piece)
-            for piece, (engine, a, b) in zip(staged, pieces):
-                if engine == "gpsimd":
-                    nc.gpsimd.tensor_scalar(slots[:, a:b, t], piece[:], 1.0, 0.0, MULT, ADD)
-                elif t == PACK - 1 and b == S:
-                    for c in range(a, b, PLACE):
-                        nc.scalar.copy(slots[:, c : c + PLACE, t], piece[:, c - a : c - a + PLACE])
-                else:
+                nc.vector.tensor_copy(ts_picked[:], looked_up(ts_window, 0, S))
+            if t < 2:
+                for a, b in EARLY_RUNS:
+                    place_on_gpsimd(t, a, b, gather_on_scalar(t, a, b, BF16))
+            else:
+                a, b = LATE_ON_GPSIMD
+                place_on_gpsimd(t, a, b, gather_on_scalar(t, a, b, F32))
+                pieces = [gather_on_scalar(t, a, b, BF16) for a, b in LATE_ON_SCALAR]
+                for piece, (a, b) in zip(pieces, LATE_ON_SCALAR):
                     nc.scalar.copy(slots[:, a:b, t], piece[:])
 
         w_grouped = keep.tile([P, N, PACK], BF16, name="w_grouped", align_bytes=64)
@@ -104,7 +112,7 @@ def tile_picked_tokscale_none_l_kernel(tc, xT, tscale, cscale, w1, offs, out):
                 scales=scales[:],
                 in_=grouped[:, at * PACK : (at + width) * PACK],
             )
-            for part in range(width // PART):
+            for part in sorted(range(width // PART), key=lambda q: (at // PART + q == ASIDE, -q)):
                 sub = slice(part * PART, (part + 1) * PART)
                 acc = psum.tile([P, PART], F32, name=f"acc{len(accs)}", tag=f"bank{len(accs)}")
                 nc.tensor.matmul_mx(
@@ -132,5 +140,4 @@ def tile_picked_tokscale_none_l_kernel(tc, xT, tscale, cscale, w1, offs, out):
             for first, last in STORES:
                 if first <= part <= last and all(q in done for q in range(first, last + 1)):
                     run = slice(first * PART, (last + 1) * PART)
-                    queue = nc.scalar if first <= ASIDE <= last else nc.sync
-                    queue.dma_start(out[:, run], result[:, run])
+                    nc.sync.dma_start(out[:, run], result[:, run])

@@ -18,6 +18,7 @@ COPY = mybir.ActivationFunctionType.Copy
 P = 128
 PACK = 4
 PER_PART = T // P
+RUN_STEP = P // PER_PART
 PER_BANK = 4
 PART = 128
 ON_VECTOR = (384, 896)
@@ -36,8 +37,9 @@ def tile_picked_tokscale_none_l_kernel(tc, xT, tscale, cscale, w1, offs, out):
         tc.psum_pool(name="psum", bufs=1) as psum,
     ):
         offsets = keep.tile([P, S // 16], U16, name="offsets")
-        ts_rows = keep.tile([P, PER_PART], F32, name="ts_rows")
-        nc.scalar.dma_start(ts_rows[:], tscale[0, :].rearrange("(n m) -> n m", m=PER_PART))
+        ts_runs = keep.tile([P, P], F32, name="ts_runs")
+        nc.gpsimd.memset(ts_runs[:], 0.0)
+        nc.scalar.dma_start(ts_runs[0:P:RUN_STEP, :], tscale[0, :].rearrange("(q c) -> q c", c=P))
         x_rows = xT.rearrange("(p t) c -> t p c", t=PACK)
         planes = [keep.tile([P, T], F32, name=f"plane{t}") for t in range(PACK)]
         for t in range(PACK):
@@ -51,21 +53,20 @@ def tile_picked_tokscale_none_l_kernel(tc, xT, tscale, cscale, w1, offs, out):
 
         ident = keep.tile([P, P], F32, name="ident")
         make_identity(nc, ident[:])
+        turned = psum.tile([P, P], F32, name="turned", tag="bank7")
+        nc.tensor.transpose(turned[:], ts_runs[:], ident[:])
+        ts_cols = keep.tile([P, PER_PART], F32, name="ts_cols", tag="early", align_bytes=64)
+        nc.vector.tensor_copy(ts_cols[:], turned[:, 0:P:RUN_STEP])
         ts_window = keep.tile([P, T], F32, name="ts_window")
-        ts_view = ts_window[:].rearrange("p (n m) -> p n m", m=PER_PART)
         for b in range(PER_PART // PER_BANK):
-            bank = psum.tile([P, PER_BANK, P], F32, name=f"spread{b}", tag=f"bank{b}")
+            bank = psum.tile([P, PER_BANK * P], F32, name=f"spread{b}", tag=f"bank{b}")
             for i in range(PER_BANK):
-                m = b * PER_BANK + i
-                nc.tensor.transpose(bank[:, i, :], ts_rows[:, m : m + 1].to_broadcast([P, P]), ident[:])
-            spread = ts_view[:, :, b * PER_BANK : (b + 1) * PER_BANK]
-            if b % 2 == 0:
-                nc.vector.tensor_copy(spread, bank[:].rearrange("p i n -> p n i"))
-            else:
-                nc.scalar.copy(spread, bank[:].rearrange("p i n -> p n i"))
+                q = b * PER_BANK + i
+                nc.tensor.transpose(bank[:, i * P : (i + 1) * P], ts_cols[:, q : q + 1].to_broadcast([P, P]), ident[:])
+            nc.vector.tensor_copy(ts_window[:, b * PER_BANK * P : (b + 1) * PER_BANK * P], bank[:])
 
         ts_picked = keep.tile([P, S], F32, name="ts_picked")
-        grouped = keep.tile([P, S * PACK], BF16, name="grouped", align_bytes=64)
+        grouped = keep.tile([P, S * PACK], BF16, name="grouped", tag="early", align_bytes=64)
         slots = grouped[:].rearrange("p (n t) -> p n t", t=PACK)
 
         def looked_up(window, a, b):

@@ -21,6 +21,7 @@ PER_PART = T // P
 RUN_STEP = P // PER_PART
 PER_BANK = 4
 PART = 128
+BURST = 256
 ON_VECTOR = (384, 896)
 EARLY_RUNS = ((0, 384), (896, 1024))
 LATE_ON_GPSIMD = (128, 192)
@@ -36,17 +37,17 @@ def tile_picked_tokscale_none_l_kernel(tc, xT, tscale, cscale, w1, offs, out):
         tc.tile_pool(name="keep", bufs=1) as keep,
         tc.psum_pool(name="psum", bufs=1) as psum,
     ):
-        offsets = keep.tile([P, S // 16], U16, name="offsets")
-        ts_runs = keep.tile([P, P], F32, name="ts_runs")
+        offsets = keep.tile([P, S // 16], U16, name="offsets", align_bytes=BURST)
+        ts_runs = keep.tile([P, P], F32, name="ts_runs", align_bytes=BURST)
         nc.gpsimd.memset(ts_runs[:], 0.0)
         nc.scalar.dma_start(ts_runs[0:P:RUN_STEP, :], tscale[0, :].rearrange("(q c) -> q c", c=P))
         x_rows = xT.rearrange("(p t) c -> t p c", t=PACK)
-        planes = [keep.tile([P, T], F32, name=f"plane{t}") for t in range(PACK)]
+        planes = [keep.tile([P, T], F32, name=f"plane{t}", align_bytes=BURST) for t in range(PACK)]
         for t in range(PACK):
             nc.sync.dma_start(planes[t][:], x_rows[t])
             if t == 0:
                 nc.sync.dma_start(offsets[:], offs)
-        w_raw = keep.tile([P, PACK, N], F32, name="w_raw", tag="shared", align_bytes=64)
+        w_raw = keep.tile([P, PACK, N], F32, name="w_raw", tag="shared", align_bytes=BURST)
         nc.sync.dma_start(w_raw[:], w1.rearrange("(p t) n -> p t n", t=PACK))
         cs = keep.tile([P, 1], F32, name="cs")
         nc.sync.dma_start(cs[:], cscale)
@@ -103,7 +104,7 @@ def tile_picked_tokscale_none_l_kernel(tc, xT, tscale, cscale, w1, offs, out):
         nc.vector.quantize_mx(
             out=w_codes[:].bitcast(FP8X4), scales=w_scales[:], in_=w_grouped[:].rearrange("p n t -> p (n t)")
         )
-        all_codes = keep.tile([P, S], U32, name="all_codes", tag="shared", align_bytes=64)
+        all_codes = keep.tile([P, S], U32, name="all_codes", tag="shared", align_bytes=BURST)
         accs = []
         for at, width in QUANTS:
             codes = all_codes[:, at : at + width]
@@ -127,7 +128,7 @@ def tile_picked_tokscale_none_l_kernel(tc, xT, tscale, cscale, w1, offs, out):
                 )
                 accs.append((acc, at // PART + part))
 
-        result = keep.tile([P, S], F32, name="result")
+        result = keep.tile([P, S], F32, name="result", align_bytes=BURST)
         done = set()
         for acc, part in accs:
             cols = slice(part * PART, (part + 1) * PART)

@@ -25,10 +25,10 @@ BURST = 256
 ON_VECTOR = (384, 896)
 EARLY_RUNS = ((0, 384), (896, 1024))
 LATE_ON_GPSIMD = (128, 192)
-LATE_ON_SCALAR = ((192, 384), (0, 128), (896, 1024))
-QUANTS = ((640, 256), (384, 256), (128, 256), (0, 128), (896, 128))
+LATE_ON_SCALAR = ((0, 128), (192, 384), (896, 1024))
+QUANTS = ((0, 128), (640, 256), (384, 256), (128, 256), (896, 128))
 ASIDE = 6
-STORES = ((5, 5), (4, 4), (2, 3), (0, 1), (6, 7))
+STORES = ((0, 0), (5, 5), (3, 4), (1, 2), (6, 7))
 
 
 def tile_picked_tokscale_none_l_kernel(tc, xT, tscale, cscale, w1, offs, out):
@@ -92,9 +92,11 @@ def tile_picked_tokscale_none_l_kernel(tc, xT, tscale, cscale, w1, offs, out):
             else:
                 a, b = LATE_ON_GPSIMD
                 place_on_gpsimd(t, a, b, gather_on_scalar(t, a, b, F32))
-                pieces = [gather_on_scalar(t, a, b, BF16) for a, b in LATE_ON_SCALAR]
-                for piece, (a, b) in zip(pieces, LATE_ON_SCALAR):
-                    nc.scalar.copy(slots[:, a:b, t], piece[:])
+                pieces = [gather_on_scalar(t, a, b, BF16) for a, b in LATE_ON_SCALAR[:2]]
+                for i, (a, b) in enumerate(LATE_ON_SCALAR):
+                    nc.scalar.copy(slots[:, a:b, t], pieces[i][:])
+                    if i == 0:
+                        pieces.append(gather_on_scalar(t, *LATE_ON_SCALAR[2], BF16))
 
         w_grouped = keep.tile([P, N, PACK], BF16, name="w_grouped", align_bytes=64)
         nc.gpsimd.tensor_scalar(w_grouped[:], w_raw[:].rearrange("p t n -> p n t"), 1.0, 0.0, MULT, ADD)

@@ -22,10 +22,10 @@ RUN_STEP = P // PER_PART
 PER_BANK = 4
 PART = 128
 BURST = 256
-ON_VECTOR = (384, 896)
-EARLY_RUNS = ((0, 384), (896, 1024))
+ON_VECTOR = (384, 928)
+EARLY_RUNS = ((0, 384), (928, 1024))
 LATE_ON_GPSIMD = (128, 192)
-LATE_ON_SCALAR = ((0, 128), (192, 384), (896, 1024))
+LATE_ON_SCALAR = ((0, 128), (192, 384), (928, 1024))
 QUANTS = ((0, 128), (640, 256), (384, 256), (128, 256), (896, 128))
 ASIDE = 6
 STORES = ((0, 0), (5, 5), (3, 4), (1, 2), (6, 7))
@@ -67,36 +67,48 @@ def tile_picked_tokscale_none_l_kernel(tc, xT, tscale, cscale, w1, offs, out):
             nc.vector.tensor_copy(ts_window[:, b * PER_BANK * P : (b + 1) * PER_BANK * P], bank[:])
 
         ts_picked = keep.tile([P, S], F32, name="ts_picked")
-        grouped = keep.tile([P, S * PACK], BF16, name="grouped", tag="early", align_bytes=64)
-        slots = grouped[:].rearrange("p (n t) -> p n t", t=PACK)
+        stretches = ((0, ON_VECTOR[0], "low"), (ON_VECTOR[0], S, "early"))
+        grouped = [
+            (a, b, keep.tile([P, (b - a) * PACK], BF16, name=f"grouped{a}", tag=tag, align_bytes=64))
+            for a, b, tag in stretches
+        ]
+
+        def entries(a, b):
+            start, tile = [(lo, tile) for lo, hi, tile in grouped if lo <= a and b <= hi][0]
+            return tile[:, (a - start) * PACK : (b - start) * PACK]
+
+        def slot(t, a, b):
+            return entries(a, b).rearrange("p (n t) -> p n t", t=PACK)[:, :, t]
 
         def looked_up(window, a, b):
             return window[:].indirect(offsets[:, a // 16 : b // 16])
 
-        def gather_on_scalar(t, a, b, dtype):
-            piece = keep.tile([P, b - a], dtype, name=f"piece{t}_{a}")
+        def gather_on_scalar(t, a, b, tag=None):
+            dtype = BF16 if b - a >= PART else F32
+            piece = keep.tile([P, b - a], dtype, name=f"piece{t}_{a}", tag=tag or f"piece{t}_{a}")
             nc.scalar.activation(piece[:], looked_up(planes[t], a, b), COPY)
             return piece
 
         def place_on_gpsimd(t, a, b, piece):
-            nc.gpsimd.tensor_scalar(slots[:, a:b, t], piece[:], 1.0, 0.0, MULT, ADD)
+            nc.gpsimd.tensor_scalar(slot(t, a, b), piece[:], 1.0, 0.0, MULT, ADD)
 
         for t in range(PACK):
             a, b = ON_VECTOR
-            nc.vector.tensor_copy(slots[:, a:b, t], looked_up(planes[t], a, b))
+            nc.vector.tensor_copy(slot(t, a, b), looked_up(planes[t], a, b))
             if t == 0:
                 nc.vector.tensor_copy(ts_picked[:], looked_up(ts_window, 0, S))
             if t < 2:
                 for a, b in EARLY_RUNS:
-                    place_on_gpsimd(t, a, b, gather_on_scalar(t, a, b, BF16))
+                    place_on_gpsimd(t, a, b, gather_on_scalar(t, a, b))
             else:
+                turn = "turn" if t == PACK - 1 else None
                 a, b = LATE_ON_GPSIMD
-                place_on_gpsimd(t, a, b, gather_on_scalar(t, a, b, F32))
-                pieces = [gather_on_scalar(t, a, b, BF16) for a, b in LATE_ON_SCALAR[:2]]
+                place_on_gpsimd(t, a, b, gather_on_scalar(t, a, b, turn))
+                pieces = [gather_on_scalar(t, a, b) for a, b in LATE_ON_SCALAR[:2]]
                 for i, (a, b) in enumerate(LATE_ON_SCALAR):
-                    nc.scalar.copy(slots[:, a:b, t], pieces[i][:])
+                    nc.scalar.copy(slot(t, a, b), pieces[i][:])
                     if i == 0:
-                        pieces.append(gather_on_scalar(t, *LATE_ON_SCALAR[2], BF16))
+                        pieces.append(gather_on_scalar(t, *LATE_ON_SCALAR[2], turn))
 
         w_grouped = keep.tile([P, N, PACK], BF16, name="w_grouped", align_bytes=64)
         nc.gpsimd.tensor_scalar(w_grouped[:], w_raw[:].rearrange("p t n -> p n t"), 1.0, 0.0, MULT, ADD)
@@ -114,7 +126,7 @@ def tile_picked_tokscale_none_l_kernel(tc, xT, tscale, cscale, w1, offs, out):
             nc.vector.quantize_mx(
                 out=codes.bitcast(FP8X4),
                 scales=scales[:],
-                in_=grouped[:, at * PACK : (at + width) * PACK],
+                in_=entries(at, at + width),
             )
             for part in sorted(range(width // PART), key=lambda q: (at // PART + q == ASIDE, -q)):
                 sub = slice(part * PART, (part + 1) * PART)

@@ -22,10 +22,10 @@ RUN_STEP = P // PER_PART
 PER_BANK = 4
 PART = 128
 BURST = 256
-ON_VECTOR = (384, 928)
-EARLY_RUNS = ((0, 384), (928, 1024))
+ON_VECTOR = (384, 896)
+EARLY_RUNS = ((0, 384), (896, 1024))
 LATE_ON_GPSIMD = (128, 192)
-LATE_ON_SCALAR = ((0, 128), (192, 384), (928, 1024))
+LATE_ON_SCALAR = ((0, 128), (192, 384), (896, 1024))
 QUANTS = ((0, 128), (640, 256), (384, 256), (128, 256), (896, 128))
 ASIDE = 6
 STORES = ((0, 0), (5, 5), (3, 4), (1, 2), (6, 7))
@@ -119,15 +119,30 @@ def tile_picked_tokscale_none_l_kernel(tc, xT, tscale, cscale, w1, offs, out):
             out=w_codes[:].bitcast(FP8X4), scales=w_scales[:], in_=w_grouped[:].rearrange("p n t -> p (n t)")
         )
         all_codes = keep.tile([P, S], U32, name="all_codes", tag="shared", align_bytes=BURST)
+        result = keep.tile([P, S], F32, name="result", align_bytes=BURST)
         accs = []
+        done = set()
+
+        def finish(acc, part):
+            cols = slice(part * PART, (part + 1) * PART)
+            if part == ASIDE:
+                aside = keep.tile([P, PART], F32, name="aside")
+                nc.scalar.activation(aside[:], acc[:], COPY, scale=cs[:, 0:1])
+                nc.gpsimd.tensor_tensor(result[:, cols], aside[:], ts_picked[:, cols], MULT)
+            else:
+                nc.vector.scalar_tensor_tensor(result[:, cols], ts_picked[:, cols], cs[:, 0:1], acc[:], MULT, MULT)
+            done.add(part)
+            for first, last in STORES:
+                if first <= part <= last and all(q in done for q in range(first, last + 1)):
+                    run = slice(first * PART, (last + 1) * PART)
+                    nc.sync.dma_start(out[:, run], result[:, run])
+
         for at, width in QUANTS:
+            if (at, width) == QUANTS[-1]:
+                finish(*accs[0])
             codes = all_codes[:, at : at + width]
             scales = keep.tile([P, width], U8, name=f"scales{at}", align_bytes=64)
-            nc.vector.quantize_mx(
-                out=codes.bitcast(FP8X4),
-                scales=scales[:],
-                in_=entries(at, at + width),
-            )
+            nc.vector.quantize_mx(out=codes.bitcast(FP8X4), scales=scales[:], in_=entries(at, at + width))
             for part in sorted(range(width // PART), key=lambda q: (at // PART + q == ASIDE, -q)):
                 sub = slice(part * PART, (part + 1) * PART)
                 acc = psum.tile([P, PART], F32, name=f"acc{len(accs)}", tag=f"bank{len(accs)}")
@@ -141,19 +156,5 @@ def tile_picked_tokscale_none_l_kernel(tc, xT, tscale, cscale, w1, offs, out):
                     stop=True,
                 )
                 accs.append((acc, at // PART + part))
-
-        result = keep.tile([P, S], F32, name="result", align_bytes=BURST)
-        done = set()
-        for acc, part in accs:
-            cols = slice(part * PART, (part + 1) * PART)
-            if part == ASIDE:
-                aside = keep.tile([P, PART], F32, name="aside")
-                nc.scalar.activation(aside[:], acc[:], COPY, scale=cs[:, 0:1])
-                nc.gpsimd.tensor_tensor(result[:, cols], aside[:], ts_picked[:, cols], MULT)
-            else:
-                nc.vector.scalar_tensor_tensor(result[:, cols], ts_picked[:, cols], cs[:, 0:1], acc[:], MULT, MULT)
-            done.add(part)
-            for first, last in STORES:
-                if first <= part <= last and all(q in done for q in range(first, last + 1)):
-                    run = slice(first * PART, (last + 1) * PART)
-                    nc.sync.dma_start(out[:, run], result[:, run])
+        for acc, part in accs[1:]:
+            finish(acc, part)

@@ -115,9 +115,7 @@ def tile_picked_tokscale_none_l_kernel(tc, xT, tscale, cscale, w1, offs, out):
         w_codes = keep.tile([P, N], U32, name="w_codes", align_bytes=64)
         w_scales = keep.tile([P, N], U8, name="w_scales", align_bytes=64)
 
-        nc.vector.quantize_mx(
-            out=w_codes[:].bitcast(FP8X4), scales=w_scales[:], in_=w_grouped[:].rearrange("p n t -> p (n t)")
-        )
+        first_codes = keep.tile([P, PART], U32, name="first_codes", align_bytes=64)
         all_codes = keep.tile([P, S], U32, name="all_codes", tag="shared", align_bytes=BURST)
         result = keep.tile([P, S], F32, name="result", align_bytes=BURST)
         accs = []
@@ -140,9 +138,13 @@ def tile_picked_tokscale_none_l_kernel(tc, xT, tscale, cscale, w1, offs, out):
         for at, width in QUANTS:
             if (at, width) == QUANTS[-1]:
                 finish(*accs[0])
-            codes = all_codes[:, at : at + width]
+            codes = first_codes[:] if at == 0 else all_codes[:, at : at + width]
             scales = keep.tile([P, width], U8, name=f"scales{at}", align_bytes=64)
             nc.vector.quantize_mx(out=codes.bitcast(FP8X4), scales=scales[:], in_=entries(at, at + width))
+            if at == 0:
+                nc.vector.quantize_mx(
+                    out=w_codes[:].bitcast(FP8X4), scales=w_scales[:], in_=w_grouped[:].rearrange("p n t -> p (n t)")
+                )
             for part in sorted(range(width // PART), key=lambda q: (at // PART + q == ASIDE, -q)):
                 sub = slice(part * PART, (part + 1) * PART)
                 acc = psum.tile([P, PART], F32, name=f"acc{len(accs)}", tag=f"bank{len(accs)}")

@@ -24,8 +24,8 @@ PART = 128
 BURST = 256
 ON_VECTOR = (384, 896)
 EARLY_RUNS = ((0, 384), (896, 1024))
-LATE_ON_GPSIMD = (128, 192)
-LATE_ON_SCALAR = ((0, 128), (192, 384), (896, 1024))
+LATE_ON_GPSIMD = (128, 224)
+LATE_ON_SCALAR = ((0, 128), (224, 384), (896, 1024))
 QUANTS = ((0, 128), (640, 256), (384, 256), (128, 256), (896, 128))
 ASIDE = 6
 STORES = ((0, 0), (5, 5), (3, 4), (1, 2), (6, 7))
@@ -136,8 +136,6 @@ def tile_picked_tokscale_none_l_kernel(tc, xT, tscale, cscale, w1, offs, out):
                     nc.sync.dma_start(out[:, run], result[:, run])
 
         for at, width in QUANTS:
-            if (at, width) == QUANTS[-1]:
-                finish(*accs[0])
             codes = first_codes[:] if at == 0 else all_codes[:, at : at + width]
             scales = keep.tile([P, width], U8, name=f"scales{at}", align_bytes=64)
             nc.vector.quantize_mx(out=codes.bitcast(FP8X4), scales=scales[:], in_=entries(at, at + width))
@@ -158,5 +156,5 @@ def tile_picked_tokscale_none_l_kernel(tc, xT, tscale, cscale, w1, offs, out):
                     stop=True,
                 )
                 accs.append((acc, at // PART + part))
-        for acc, part in accs[1:]:
+        for acc, part in accs:
             finish(acc, part)

@@ -12,42 +12,42 @@ U16 = mybir.dt.uint16
 U8 = mybir.dt.uint8
 FP8X4 = mybir.dt.float8_e4m3fn_x4
 MULT = mybir.AluOpType.mult
-ADD = mybir.AluOpType.add
 COPY = mybir.ActivationFunctionType.Copy
 
 P = 128
 PACK = 4
-PER_PART = T // P
-RUN_STEP = P // PER_PART
+RUNS = T // P
 PER_BANK = 4
 PART = 128
+PARTS = S // PART
 BURST = 256
-ON_VECTOR = (384, 896)
-EARLY_RUNS = ((0, 384), (896, 1024))
-LATE_ON_GPSIMD = (128, 224)
-LATE_ON_SCALAR = ((0, 128), (224, 384), (896, 1024))
-QUANTS = ((0, 128), (640, 256), (384, 256), (128, 256), (896, 128))
-ASIDE = 6
-STORES = ((0, 0), (5, 5), (3, 4), (1, 2), (6, 7))
+ON_VECTOR = (256, 384)
+SCALES_ON_SCALAR = 4
+STORES = ((0, 1), (2, 3), (4, 5), (6, 6), (7, 7))
+TAIL = ("q0", "weave", "place", "qw", "q1", "q2", "q3", "q4", "q5", "m0", "m1", "q6", "m2", "m3", "q7", "m4", "m5", "m6", "m7")
+OVER_WEIGHTS = (1, 2, 3, 4, 5)
+CODES_OVER = {6: "scale0", 7: "scale2"}
 
 
 def tile_picked_tokscale_none_l_kernel(tc, xT, tscale, cscale, w1, offs, out):
     nc = tc.nc
     with (
         tc.tile_pool(name="keep", bufs=1) as keep,
+        tc.tile_pool(name="shared", bufs=1) as shared,
         tc.psum_pool(name="psum", bufs=1) as psum,
     ):
         offsets = keep.tile([P, S // 16], U16, name="offsets", align_bytes=BURST)
         ts_runs = keep.tile([P, P], F32, name="ts_runs", align_bytes=BURST)
-        nc.gpsimd.memset(ts_runs[:], 0.0)
-        nc.scalar.dma_start(ts_runs[0:P:RUN_STEP, :], tscale[0, :].rearrange("(q c) -> q c", c=P))
+        nc.scalar.dma_start(ts_runs[0:RUNS, :], tscale[0, :].rearrange("(q c) -> q c", c=P))
+        nc.gpsimd.memset(ts_runs[32:64, :], 0.0)
+        nc.gpsimd.memset(ts_runs[64:P, :], 0.0)
         x_rows = xT.rearrange("(p t) c -> t p c", t=PACK)
         planes = [keep.tile([P, T], F32, name=f"plane{t}", align_bytes=BURST) for t in range(PACK)]
         for t in range(PACK):
             nc.sync.dma_start(planes[t][:], x_rows[t])
             if t == 0:
                 nc.sync.dma_start(offsets[:], offs)
-        w_raw = keep.tile([P, PACK, N], F32, name="w_raw", tag="shared", align_bytes=BURST)
+        w_raw = shared.tile([P, PACK, N], F32, name="w_raw", align_bytes=BURST, offset=0)
         nc.sync.dma_start(w_raw[:], w1.rearrange("(p t) n -> p t n", t=PACK))
         cs = keep.tile([P, 1], F32, name="cs")
         nc.sync.dma_start(cs[:], cscale)
@@ -56,105 +56,101 @@ def tile_picked_tokscale_none_l_kernel(tc, xT, tscale, cscale, w1, offs, out):
         make_identity(nc, ident[:])
         turned = psum.tile([P, P], F32, name="turned", tag="bank7")
         nc.tensor.transpose(turned[:], ts_runs[:], ident[:])
-        ts_cols = keep.tile([P, PER_PART], F32, name="ts_cols", tag="early", align_bytes=64)
-        nc.vector.tensor_copy(ts_cols[:], turned[:, 0:P:RUN_STEP])
+        ts_cols = keep.tile([P, RUNS], F32, name="ts_cols")
+        nc.vector.tensor_copy(ts_cols[:], turned[:, 0:RUNS])
         ts_window = keep.tile([P, T], F32, name="ts_window")
-        for b in range(PER_PART // PER_BANK):
+        for b in range(RUNS // PER_BANK):
             bank = psum.tile([P, PER_BANK * P], F32, name=f"spread{b}", tag=f"bank{b}")
             for i in range(PER_BANK):
                 q = b * PER_BANK + i
                 nc.tensor.transpose(bank[:, i * P : (i + 1) * P], ts_cols[:, q : q + 1].to_broadcast([P, P]), ident[:])
             nc.vector.tensor_copy(ts_window[:, b * PER_BANK * P : (b + 1) * PER_BANK * P], bank[:])
 
-        ts_picked = keep.tile([P, S], F32, name="ts_picked")
-        stretches = ((0, ON_VECTOR[0], "low"), (ON_VECTOR[0], S, "early"))
-        grouped = [
-            (a, b, keep.tile([P, (b - a) * PACK], BF16, name=f"grouped{a}", tag=tag, align_bytes=64))
-            for a, b, tag in stretches
-        ]
-
-        def entries(a, b):
-            start, tile = [(lo, tile) for lo, hi, tile in grouped if lo <= a and b <= hi][0]
-            return tile[:, (a - start) * PACK : (b - start) * PACK]
-
-        def slot(t, a, b):
-            return entries(a, b).rearrange("p (n t) -> p n t", t=PACK)[:, :, t]
-
         def looked_up(window, a, b):
             return window[:].indirect(offsets[:, a // 16 : b // 16])
 
-        def gather_on_scalar(t, a, b, tag=None):
-            dtype = BF16 if b - a >= PART else F32
-            piece = keep.tile([P, b - a], dtype, name=f"piece{t}_{a}", tag=tag or f"piece{t}_{a}")
-            nc.scalar.activation(piece[:], looked_up(planes[t], a, b), COPY)
-            return piece
+        token_scale = []
+        for part in range(SCALES_ON_SCALAR):
+            tile = keep.tile([P, PART], F32, name=f"scale{part}", tag=f"scale{part}", align_bytes=BURST)
+            nc.scalar.activation(tile[:], looked_up(ts_window, part * PART, (part + 1) * PART), COPY)
+            token_scale.append(tile[:])
+        first = SCALES_ON_SCALAR * PART
+        rest = keep.tile([P, S - first], F32, name="scale_rest")
+        nc.vector.tensor_copy(rest[:], looked_up(ts_window, first, S))
+        token_scale.extend(rest[:, i * PART : (i + 1) * PART] for i in range(PARTS - SCALES_ON_SCALAR))
 
-        def place_on_gpsimd(t, a, b, piece):
-            nc.gpsimd.tensor_scalar(slot(t, a, b), piece[:], 1.0, 0.0, MULT, ADD)
+        grouped = keep.tile([P, S * PACK], BF16, name="grouped", align_bytes=64)
 
+        def slot(t, a, b):
+            return grouped[:, a * PACK : b * PACK].rearrange("p (n t) -> p n t", t=PACK)[:, :, t]
+
+        low, high = ON_VECTOR
         for t in range(PACK):
-            a, b = ON_VECTOR
-            nc.vector.tensor_copy(slot(t, a, b), looked_up(planes[t], a, b))
-            if t == 0:
-                nc.vector.tensor_copy(ts_picked[:], looked_up(ts_window, 0, S))
-            if t < 2:
-                for a, b in EARLY_RUNS:
-                    place_on_gpsimd(t, a, b, gather_on_scalar(t, a, b))
+            piece = keep.tile([P, high - low], BF16, name=f"piece{t}")
+            nc.vector.tensor_copy(piece[:], looked_up(planes[t], low, high))
+            if t < PACK - 1:
+                nc.vector.tensor_copy(slot(t, low, high), piece[:])
+                runs = [(a, b) for a, b in ((0, low), (high, S)) if a < b]
             else:
-                turn = "turn" if t == PACK - 1 else None
-                a, b = LATE_ON_GPSIMD
-                place_on_gpsimd(t, a, b, gather_on_scalar(t, a, b, turn))
-                pieces = [gather_on_scalar(t, a, b) for a, b in LATE_ON_SCALAR[:2]]
-                for i, (a, b) in enumerate(LATE_ON_SCALAR):
-                    nc.scalar.copy(slot(t, a, b), pieces[i][:])
-                    if i == 0:
-                        pieces.append(gather_on_scalar(t, *LATE_ON_SCALAR[2], turn))
+                runs = ((0, 128), (128, 256), (384, 512), (512, 640), (640, 768), (768, 896), (896, 1024))
+            for a, b in runs:
+                nc.scalar.activation(slot(t, a, b), looked_up(planes[t], a, b), COPY)
 
         w_grouped = keep.tile([P, N, PACK], BF16, name="w_grouped", align_bytes=64)
-        nc.gpsimd.tensor_scalar(w_grouped[:], w_raw[:].rearrange("p t n -> p n t"), 1.0, 0.0, MULT, ADD)
         w_codes = keep.tile([P, N], U32, name="w_codes", align_bytes=64)
         w_scales = keep.tile([P, N], U8, name="w_scales", align_bytes=64)
-
-        first_codes = keep.tile([P, PART], U32, name="first_codes", align_bytes=64)
-        all_codes = keep.tile([P, S], U32, name="all_codes", tag="shared", align_bytes=BURST)
         result = keep.tile([P, S], F32, name="result", align_bytes=BURST)
-        accs = []
-        done = set()
+        quantised = {}
+        products = {}
 
-        def finish(acc, part):
-            cols = slice(part * PART, (part + 1) * PART)
-            if part == ASIDE:
-                aside = keep.tile([P, PART], F32, name="aside")
-                nc.scalar.activation(aside[:], acc[:], COPY, scale=cs[:, 0:1])
-                nc.gpsimd.tensor_tensor(result[:, cols], aside[:], ts_picked[:, cols], MULT)
-            else:
-                nc.vector.scalar_tensor_tensor(result[:, cols], ts_picked[:, cols], cs[:, 0:1], acc[:], MULT, MULT)
-            done.add(part)
-            for first, last in STORES:
-                if first <= part <= last and all(q in done for q in range(first, last + 1)):
-                    run = slice(first * PART, (last + 1) * PART)
-                    nc.sync.dma_start(out[:, run], result[:, run])
+        def multiply(part):
+            codes, scales = quantised[part]
+            acc = psum.tile([P, PART], F32, name=f"acc{part}", tag=f"bank{part}")
+            nc.tensor.matmul_mx(
+                out=acc[:],
+                lhsT=w_codes[:].bitcast(FP8X4),
+                lhsT_scale=w_scales[:],
+                rhs=codes.bitcast(FP8X4),
+                rhs_scale=scales,
+                start=True,
+                stop=True,
+            )
+            products[part] = acc
 
-        for at, width in QUANTS:
-            codes = first_codes[:] if at == 0 else all_codes[:, at : at + width]
-            scales = keep.tile([P, width], U8, name=f"scales{at}", align_bytes=64)
-            nc.vector.quantize_mx(out=codes.bitcast(FP8X4), scales=scales[:], in_=entries(at, at + width))
-            if at == 0:
+        weights_ready = []
+        for step in TAIL:
+            if step == "weave":
+                nc.vector.tensor_copy(w_grouped[:], w_raw[:].rearrange("p t n -> p n t"))
+            elif step == "place":
+                nc.vector.tensor_copy(slot(PACK - 1, low, high), piece[:])
+            elif step == "qw":
                 nc.vector.quantize_mx(
                     out=w_codes[:].bitcast(FP8X4), scales=w_scales[:], in_=w_grouped[:].rearrange("p n t -> p (n t)")
                 )
-            for part in sorted(range(width // PART), key=lambda q: (at // PART + q == ASIDE, -q)):
-                sub = slice(part * PART, (part + 1) * PART)
-                acc = psum.tile([P, PART], F32, name=f"acc{len(accs)}", tag=f"bank{len(accs)}")
-                nc.tensor.matmul_mx(
-                    out=acc[:],
-                    lhsT=w_codes[:].bitcast(FP8X4),
-                    lhsT_scale=w_scales[:],
-                    rhs=codes[:, sub].bitcast(FP8X4),
-                    rhs_scale=scales[:, sub],
-                    start=True,
-                    stop=True,
-                )
-                accs.append((acc, at // PART + part))
-        for acc, part in accs:
-            finish(acc, part)
+                weights_ready.append(True)
+                for part in quantised:
+                    multiply(part)
+            elif step[0] == "q":
+                parts = [int(c) for c in step[1:]]
+                width = len(parts) * PART
+                tag = CODES_OVER.get(parts[0], f"codes{parts[0]}")
+                codes = keep.tile([P, width], U32, name=f"codes{parts[0]}", tag=tag, align_bytes=BURST)
+                name = f"scales{parts[0]}"
+                if parts[0] in OVER_WEIGHTS:
+                    at = OVER_WEIGHTS.index(parts[0]) * BURST
+                    scales = shared.tile([P, width], U8, name=name, align_bytes=BURST, offset=at)
+                else:
+                    scales = keep.tile([P, width], U8, name=name, align_bytes=64)
+                at = parts[0] * PART * PACK
+                nc.vector.quantize_mx(out=codes[:].bitcast(FP8X4), scales=scales[:], in_=grouped[:, at : at + width * PACK])
+                for i, part in enumerate(parts):
+                    quantised[part] = (codes[:, i * PART : (i + 1) * PART], scales[:, i * PART : (i + 1) * PART])
+                    if weights_ready:
+                        multiply(part)
+            else:
+                part = int(step[1])
+                cols = slice(part * PART, (part + 1) * PART)
+                nc.vector.scalar_tensor_tensor(result[:, cols], token_scale[part], cs[:, 0:1], products[part][:], MULT, MULT)
+                for a, b in STORES:
+                    if part == b:
+                        nc.sync.dma_start(out[:, a * PART : (b + 1) * PART], result[:, a * PART : (b + 1) * PART])

@@ -17,16 +17,47 @@ COPY = mybir.ActivationFunctionType.Copy
 P = 128
 PACK = 4
 RUNS = T // P
+RUN_STEP = P // RUNS
 PER_BANK = 4
-PART = 128
-PARTS = S // PART
 BURST = 256
 ON_VECTOR = (256, 384)
-SCALES_ON_SCALAR = 4
-STORES = ((0, 1), (2, 3), (4, 5), (6, 6), (7, 7))
-TAIL = ("q0", "weave", "place", "qw", "q1", "q2", "q3", "q4", "q5", "m0", "m1", "q6", "m2", "m3", "q7", "m4", "m5", "m6", "m7")
-OVER_WEIGHTS = (1, 2, 3, 4, 5)
-CODES_OVER = {6: "scale0", 7: "scale2"}
+VECTOR_PIECES = ((256, 384),)
+LAST_ON_SCALAR = ((0, 128), (128, 256), (384, 512), (512, 640), (640, 768), (768, 896), (896, 1024),)
+SCALES_ON_SCALAR = ()
+SCALES_ON_VECTOR = ((0, 1024),)
+STORES = ((0, 256), (256, 512), (512, 640), (640, 896), (896, 1024),)
+TAIL = (
+    ("quantise", 0, 128, None),
+    ("weave", 0, 0, None),
+    ("place", 256, 384, None),
+    ("weights", 0, 0, None),
+    ("product", 0, 128, None),
+    ("quantise", 128, 256, None),
+    ("product", 128, 256, None),
+    ("quantise", 256, 384, None),
+    ("product", 256, 384, None),
+    ("quantise", 384, 512, None),
+    ("product", 384, 512, None),
+    ("quantise", 512, 640, None),
+    ("product", 512, 640, None),
+    ("scale", 0, 128, None),
+    ("quantise", 640, 768, None),
+    ("product", 640, 768, None),
+    ("scale", 128, 256, None),
+    ("quantise", 768, 896, None),
+    ("product", 768, 896, None),
+    ("scale", 256, 384, None),
+    ("scale", 384, 512, None),
+    ("quantise", 896, 960, None),
+    ("product", 896, 960, None),
+    ("quantise", 960, 1024, None),
+    ("product", 960, 1024, None),
+    ("scale", 512, 640, None),
+    ("scale", 640, 768, None),
+    ("scale", 768, 896, None),
+    ("scale", 896, 960, None),
+    ("scale", 960, 1024, None),
+)
 
 
 def tile_picked_tokscale_none_l_kernel(tc, xT, tscale, cscale, w1, offs, out):
@@ -38,9 +69,8 @@ def tile_picked_tokscale_none_l_kernel(tc, xT, tscale, cscale, w1, offs, out):
     ):
         offsets = keep.tile([P, S // 16], U16, name="offsets", align_bytes=BURST)
         ts_runs = keep.tile([P, P], F32, name="ts_runs", align_bytes=BURST)
-        nc.scalar.dma_start(ts_runs[0:RUNS, :], tscale[0, :].rearrange("(q c) -> q c", c=P))
-        nc.gpsimd.memset(ts_runs[32:64, :], 0.0)
-        nc.gpsimd.memset(ts_runs[64:P, :], 0.0)
+        nc.vector.memset(ts_runs[:], 0.0)
+        nc.scalar.dma_start(ts_runs[0:P:RUN_STEP, :], tscale[0, :].rearrange("(q c) -> q c", c=P))
         x_rows = xT.rearrange("(p t) c -> t p c", t=PACK)
         planes = [keep.tile([P, T], F32, name=f"plane{t}", align_bytes=BURST) for t in range(PACK)]
         for t in range(PACK):
@@ -56,8 +86,8 @@ def tile_picked_tokscale_none_l_kernel(tc, xT, tscale, cscale, w1, offs, out):
         make_identity(nc, ident[:])
         turned = psum.tile([P, P], F32, name="turned", tag="bank7")
         nc.tensor.transpose(turned[:], ts_runs[:], ident[:])
-        ts_cols = keep.tile([P, RUNS], F32, name="ts_cols")
-        nc.vector.tensor_copy(ts_cols[:], turned[:, 0:RUNS])
+        ts_cols = keep.tile([P, RUNS], F32, name="ts_cols", tag="early", align_bytes=64)
+        nc.vector.tensor_copy(ts_cols[:], turned[:, 0:P:RUN_STEP])
         ts_window = keep.tile([P, T], F32, name="ts_window")
         for b in range(RUNS // PER_BANK):
             bank = psum.tile([P, PER_BANK * P], F32, name=f"spread{b}", tag=f"bank{b}")
@@ -70,14 +100,17 @@ def tile_picked_tokscale_none_l_kernel(tc, xT, tscale, cscale, w1, offs, out):
             return window[:].indirect(offsets[:, a // 16 : b // 16])
 
         token_scale = []
-        for part in range(SCALES_ON_SCALAR):
-            tile = keep.tile([P, PART], F32, name=f"scale{part}", tag=f"scale{part}", align_bytes=BURST)
-            nc.scalar.activation(tile[:], looked_up(ts_window, part * PART, (part + 1) * PART), COPY)
-            token_scale.append(tile[:])
-        first = SCALES_ON_SCALAR * PART
-        rest = keep.tile([P, S - first], F32, name="scale_rest")
-        nc.vector.tensor_copy(rest[:], looked_up(ts_window, first, S))
-        token_scale.extend(rest[:, i * PART : (i + 1) * PART] for i in range(PARTS - SCALES_ON_SCALAR))
+        for a, b in SCALES_ON_SCALAR + SCALES_ON_VECTOR:
+            tile = keep.tile([P, b - a], F32, name=f"scale{a}", tag=f"scale{a}", align_bytes=BURST)
+            if (a, b) in SCALES_ON_SCALAR:
+                nc.scalar.activation(tile[:], looked_up(ts_window, a, b), COPY)
+            else:
+                nc.vector.tensor_copy(tile[:], looked_up(ts_window, a, b))
+            token_scale.append((a, b, tile))
+
+        def within(tiles, a, b):
+            start, tile = [(lo, tile) for lo, hi, tile in tiles if lo <= a and b <= hi][0]
+            return tile[:, a - start : b - start]
 
         grouped = keep.tile([P, S * PACK], BF16, name="grouped", align_bytes=64)
 
@@ -85,72 +118,72 @@ def tile_picked_tokscale_none_l_kernel(tc, xT, tscale, cscale, w1, offs, out):
             return grouped[:, a * PACK : b * PACK].rearrange("p (n t) -> p n t", t=PACK)[:, :, t]
 
         low, high = ON_VECTOR
+        pieces = []
         for t in range(PACK):
-            piece = keep.tile([P, high - low], BF16, name=f"piece{t}")
-            nc.vector.tensor_copy(piece[:], looked_up(planes[t], low, high))
-            if t < PACK - 1:
-                nc.vector.tensor_copy(slot(t, low, high), piece[:])
-                runs = [(a, b) for a, b in ((0, low), (high, S)) if a < b]
-            else:
-                runs = ((0, 128), (128, 256), (384, 512), (512, 640), (640, 768), (768, 896), (896, 1024))
-            for a, b in runs:
-                nc.scalar.activation(slot(t, a, b), looked_up(planes[t], a, b), COPY)
+            last = t == PACK - 1
+            for a, b in VECTOR_PIECES if last else (ON_VECTOR,):
+                tag = f"piece{a}" if last else "early"
+                piece = keep.tile([P, b - a], BF16, name=f"piece{t}_{a}", tag=tag, align_bytes=64)
+                nc.vector.tensor_copy(piece[:], looked_up(planes[t], a, b))
+                if last:
+                    pieces.append((a, b, piece))
+                else:
+                    nc.vector.tensor_copy(slot(t, a, b), piece[:])
+            for a, b in LAST_ON_SCALAR if last else ((0, low), (high, S)):
+                if a < b:
+                    nc.scalar.activation(slot(t, a, b), looked_up(planes[t], a, b), COPY)
 
         w_grouped = keep.tile([P, N, PACK], BF16, name="w_grouped", align_bytes=64)
         w_codes = keep.tile([P, N], U32, name="w_codes", align_bytes=64)
         w_scales = keep.tile([P, N], U8, name="w_scales", align_bytes=64)
         result = keep.tile([P, S], F32, name="result", align_bytes=BURST)
-        quantised = {}
-        products = {}
+        all_codes = []
+        all_scales = []
+        products = []
+        over_weights = []
+        finished = []
 
-        def multiply(part):
-            codes, scales = quantised[part]
-            acc = psum.tile([P, PART], F32, name=f"acc{part}", tag=f"bank{part}")
-            nc.tensor.matmul_mx(
-                out=acc[:],
-                lhsT=w_codes[:].bitcast(FP8X4),
-                lhsT_scale=w_scales[:],
-                rhs=codes.bitcast(FP8X4),
-                rhs_scale=scales,
-                start=True,
-                stop=True,
-            )
-            products[part] = acc
-
-        weights_ready = []
-        for step in TAIL:
+        for step, a, b, over in TAIL:
             if step == "weave":
                 nc.vector.tensor_copy(w_grouped[:], w_raw[:].rearrange("p t n -> p n t"))
             elif step == "place":
-                nc.vector.tensor_copy(slot(PACK - 1, low, high), piece[:])
-            elif step == "qw":
+                nc.vector.tensor_copy(slot(PACK - 1, a, b), within(pieces, a, b))
+            elif step == "weights":
                 nc.vector.quantize_mx(
                     out=w_codes[:].bitcast(FP8X4), scales=w_scales[:], in_=w_grouped[:].rearrange("p n t -> p (n t)")
                 )
-                weights_ready.append(True)
-                for part in quantised:
-                    multiply(part)
-            elif step[0] == "q":
-                parts = [int(c) for c in step[1:]]
-                width = len(parts) * PART
-                tag = CODES_OVER.get(parts[0], f"codes{parts[0]}")
-                codes = keep.tile([P, width], U32, name=f"codes{parts[0]}", tag=tag, align_bytes=BURST)
-                name = f"scales{parts[0]}"
-                if parts[0] in OVER_WEIGHTS:
-                    at = OVER_WEIGHTS.index(parts[0]) * BURST
-                    scales = shared.tile([P, width], U8, name=name, align_bytes=BURST, offset=at)
+            elif step == "quantise":
+                codes = keep.tile([P, b - a], U32, name=f"codes{a}", align_bytes=BURST)
+                if over == "weights":
+                    at = len(over_weights) * BURST
+                    over_weights.append(a)
+                    scales = shared.tile([P, b - a], U8, name=f"scales{a}", align_bytes=BURST, offset=at)
                 else:
-                    scales = keep.tile([P, width], U8, name=name, align_bytes=64)
-                at = parts[0] * PART * PACK
-                nc.vector.quantize_mx(out=codes[:].bitcast(FP8X4), scales=scales[:], in_=grouped[:, at : at + width * PACK])
-                for i, part in enumerate(parts):
-                    quantised[part] = (codes[:, i * PART : (i + 1) * PART], scales[:, i * PART : (i + 1) * PART])
-                    if weights_ready:
-                        multiply(part)
+                    scales = keep.tile([P, b - a], U8, name=f"scales{a}", tag=over or f"scales{a}", align_bytes=BURST)
+                nc.vector.quantize_mx(out=codes[:].bitcast(FP8X4), scales=scales[:], in_=grouped[:, a * PACK : b * PACK])
+                all_codes.append((a, b, codes))
+                all_scales.append((a, b, scales))
+            elif step == "product":
+                acc = psum.tile([P, b - a], F32, name=f"acc{a}", tag=f"bank{len(products) % 8}")
+                nc.tensor.matmul_mx(
+                    out=acc[:],
+                    lhsT=w_codes[:].bitcast(FP8X4),
+                    lhsT_scale=w_scales[:],
+                    rhs=within(all_codes, a, b).bitcast(FP8X4),
+                    rhs_scale=within(all_scales, a, b),
+                    start=True,
+                    stop=True,
+                )
+                products.append((a, b, acc))
             else:
-                part = int(step[1])
-                cols = slice(part * PART, (part + 1) * PART)
-                nc.vector.scalar_tensor_tensor(result[:, cols], token_scale[part], cs[:, 0:1], products[part][:], MULT, MULT)
-                for a, b in STORES:
-                    if part == b:
-                        nc.sync.dma_start(out[:, a * PART : (b + 1) * PART], result[:, a * PART : (b + 1) * PART])
+                acc, factor = within(products, a, b), within(token_scale, a, b)
+                if step == "scale":
+                    nc.vector.scalar_tensor_tensor(result[:, a:b], factor, cs[:, 0:1], acc, MULT, MULT)
+                else:
+                    aside = keep.tile([P, b - a], F32, name=f"aside{a}")
+                    nc.scalar.activation(aside[:], acc, COPY, scale=cs[:, 0:1])
+                    nc.gpsimd.tensor_tensor(result[:, a:b], aside[:], factor, MULT)
+                finished.extend(range(a, b))
+                for first, end in STORES:
+                    if first < b and a < end and all(j in finished for j in range(first, end)):
+                        nc.sync.dma_start(out[:, first:end], result[:, first:end])

@@ -21,10 +21,10 @@ RUN_STEP = P // RUNS
 PER_BANK = 4
 BURST = 256
 ON_VECTOR = (256, 384)
-VECTOR_PIECES = ((256, 384),)
 LAST_ON_SCALAR = ((0, 128), (128, 256), (384, 512), (512, 640), (640, 768), (768, 896), (896, 1024),)
 SCALES_ON_SCALAR = ()
 SCALES_ON_VECTOR = ((0, 1024),)
+PIECE_BYTES = 256
 STORES = ((0, 256), (256, 512), (512, 640), (640, 896), (896, 1024),)
 TAIL = (
     ("quantise", 0, 128, None),
@@ -65,6 +65,7 @@ def tile_picked_tokscale_none_l_kernel(tc, xT, tscale, cscale, w1, offs, out):
     with (
         tc.tile_pool(name="keep", bufs=1) as keep,
         tc.tile_pool(name="shared", bufs=1) as shared,
+        tc.tile_pool(name="early", bufs=1) as early,
         tc.psum_pool(name="psum", bufs=1) as psum,
     ):
         offsets = keep.tile([P, S // 16], U16, name="offsets", align_bytes=BURST)
@@ -82,11 +83,11 @@ def tile_picked_tokscale_none_l_kernel(tc, xT, tscale, cscale, w1, offs, out):
         cs = keep.tile([P, 1], F32, name="cs")
         nc.sync.dma_start(cs[:], cscale)
 
-        ident = keep.tile([P, P], F32, name="ident")
+        ident = early.tile([P, P], F32, name="ident", offset=PIECE_BYTES - BURST)
         make_identity(nc, ident[:])
         turned = psum.tile([P, P], F32, name="turned", tag="bank7")
         nc.tensor.transpose(turned[:], ts_runs[:], ident[:])
-        ts_cols = keep.tile([P, RUNS], F32, name="ts_cols", tag="early", align_bytes=64)
+        ts_cols = early.tile([P, RUNS], F32, name="ts_cols", offset=3 * PIECE_BYTES - 64)
         nc.vector.tensor_copy(ts_cols[:], turned[:, 0:P:RUN_STEP])
         ts_window = keep.tile([P, T], F32, name="ts_window")
         for b in range(RUNS // PER_BANK):
@@ -118,20 +119,17 @@ def tile_picked_tokscale_none_l_kernel(tc, xT, tscale, cscale, w1, offs, out):
             return grouped[:, a * PACK : b * PACK].rearrange("p (n t) -> p n t", t=PACK)[:, :, t]
 
         low, high = ON_VECTOR
-        pieces = []
-        for t in range(PACK):
-            last = t == PACK - 1
-            for a, b in VECTOR_PIECES if last else (ON_VECTOR,):
-                tag = f"piece{a}" if last else "early"
-                piece = keep.tile([P, b - a], BF16, name=f"piece{t}_{a}", tag=tag, align_bytes=64)
-                nc.vector.tensor_copy(piece[:], looked_up(planes[t], a, b))
-                if last:
-                    pieces.append((a, b, piece))
-                else:
-                    nc.vector.tensor_copy(slot(t, a, b), piece[:])
-            for a, b in LAST_ON_SCALAR if last else ((0, low), (high, S)):
+        pieces = [early.tile([P, high - low], BF16, name=f"piece{t}", offset=t * PIECE_BYTES) for t in range(PACK)]
+        for t in range(PACK - 1):
+            nc.vector.tensor_copy(pieces[t][:], looked_up(planes[t], low, high))
+            for a, b in ((0, low), (high, S)):
                 if a < b:
                     nc.scalar.activation(slot(t, a, b), looked_up(planes[t], a, b), COPY)
+        for t in range(PACK - 1):
+            nc.vector.tensor_copy(slot(t, low, high), pieces[t][:])
+        nc.vector.tensor_copy(pieces[PACK - 1][:], looked_up(planes[PACK - 1], low, high))
+        for a, b in LAST_ON_SCALAR:
+            nc.scalar.activation(slot(PACK - 1, a, b), looked_up(planes[PACK - 1], a, b), COPY)
 
         w_grouped = keep.tile([P, N, PACK], BF16, name="w_grouped", align_bytes=64)
         w_codes = keep.tile([P, N], U32, name="w_codes", align_bytes=64)
@@ -147,7 +145,7 @@ def tile_picked_tokscale_none_l_kernel(tc, xT, tscale, cscale, w1, offs, out):
             if step == "weave":
                 nc.vector.tensor_copy(w_grouped[:], w_raw[:].rearrange("p t n -> p n t"))
             elif step == "place":
-                nc.vector.tensor_copy(slot(PACK - 1, a, b), within(pieces, a, b))
+                nc.vector.tensor_copy(slot(PACK - 1, a, b), pieces[PACK - 1][:, a - low : b - low])
             elif step == "weights":
                 nc.vector.quantize_mx(
                     out=w_codes[:].bitcast(FP8X4), scales=w_scales[:], in_=w_grouped[:].rearrange("p n t -> p (n t)")

@@ -25,7 +25,7 @@ LAST_ON_SCALAR = ((0, 128), (128, 256), (384, 512), (512, 640), (640, 768), (768
 SCALES_ON_SCALAR = ()
 SCALES_ON_VECTOR = ((0, 1024),)
 PIECE_BYTES = 256
-STORES = ((0, 256), (256, 512), (512, 640), (640, 896), (896, 1024),)
+STORES = ((0, 128), (128, 384), (384, 640), (640, 896), (896, 1024),)
 TAIL = (
     ("quantise", 0, 128, None),
     ("weave", 0, 0, None),
@@ -40,23 +40,20 @@ TAIL = (
     ("product", 384, 512, None),
     ("quantise", 512, 640, None),
     ("product", 512, 640, None),
-    ("scale", 0, 128, None),
     ("quantise", 640, 768, None),
     ("product", 640, 768, None),
-    ("scale", 128, 256, None),
+    ("scale", 0, 128, None),
     ("quantise", 768, 896, None),
     ("product", 768, 896, None),
+    ("scale", 128, 256, None),
     ("scale", 256, 384, None),
+    ("quantise", 896, 1024, None),
+    ("product", 896, 1024, None),
     ("scale", 384, 512, None),
-    ("quantise", 896, 960, None),
-    ("product", 896, 960, None),
-    ("quantise", 960, 1024, None),
-    ("product", 960, 1024, None),
     ("scale", 512, 640, None),
     ("scale", 640, 768, None),
     ("scale", 768, 896, None),
-    ("scale", 896, 960, None),
-    ("scale", 960, 1024, None),
+    ("scale", 896, 1024, None),
 )
 
 

@@ -20,27 +20,25 @@ RUNS = T // P
 RUN_STEP = P // RUNS
 PER_BANK = 4
 BURST = 256
-ON_VECTOR = (256, 384)
-LAST_ON_SCALAR = ((0, 128), (128, 256), (384, 512), (512, 640), (640, 768), (768, 896), (896, 1024),)
+ON_VECTOR = (128, 320)
+LAST_ON_SCALAR = ((0, 128), (320, 512), (512, 768), (768, 896), (896, 1024),)
 SCALES_ON_SCALAR = ()
 SCALES_ON_VECTOR = ((0, 1024),)
-PIECE_BYTES = 256
+PIECE_BYTES = 384
 STORES = ((0, 128), (128, 384), (384, 640), (640, 896), (896, 1024),)
 TAIL = (
     ("quantise", 0, 128, None),
     ("weave", 0, 0, None),
-    ("place", 256, 384, None),
+    ("place", 128, 320, None),
     ("weights", 0, 0, None),
     ("product", 0, 128, None),
     ("quantise", 128, 256, None),
     ("product", 128, 256, None),
-    ("quantise", 256, 384, None),
+    ("quantise", 256, 512, None),
     ("product", 256, 384, None),
-    ("quantise", 384, 512, None),
     ("product", 384, 512, None),
-    ("quantise", 512, 640, None),
+    ("quantise", 512, 768, None),
     ("product", 512, 640, None),
-    ("quantise", 640, 768, None),
     ("product", 640, 768, None),
     ("scale", 0, 128, None),
     ("quantise", 768, 896, None),
@@ -140,7 +138,10 @@ def tile_picked_tokscale_none_l_kernel(tc, xT, tscale, cscale, w1, offs, out):
 
         for step, a, b, over in TAIL:
             if step == "weave":
-                nc.vector.tensor_copy(w_grouped[:], w_raw[:].rearrange("p t n -> p n t"))
+                nc.vector.tensor_copy(
+                    w_grouped[:].rearrange("p (c i) t -> p c t i", i=PACK),
+                    w_raw[:].rearrange("p t (c i) -> p c t i", i=PACK),
+                )
             elif step == "place":
                 nc.vector.tensor_copy(slot(PACK - 1, a, b), pieces[PACK - 1][:, a - low : b - low])
             elif step == "weights":

@@ -25,11 +25,12 @@ LAST_ON_SCALAR = ((0, 128), (320, 512), (512, 768), (768, 896), (896, 1024),)
 SCALES_ON_SCALAR = ()
 SCALES_ON_VECTOR = ((0, 1024),)
 PIECE_BYTES = 384
+LEFT_OVER = 128
 STORES = ((0, 128), (128, 384), (384, 640), (640, 896), (896, 1024),)
 TAIL = (
-    ("quantise", 0, 128, None),
-    ("weave", 0, 0, None),
     ("place", 128, 320, None),
+    ("weave", 0, 0, None),
+    ("quantise", 0, 128, None),
     ("weights", 0, 0, None),
     ("product", 0, 128, None),
     ("quantise", 128, 256, None),
@@ -121,8 +122,10 @@ def tile_picked_tokscale_none_l_kernel(tc, xT, tscale, cscale, w1, offs, out):
                 if a < b:
                     nc.scalar.activation(slot(t, a, b), looked_up(planes[t], a, b), COPY)
         for t in range(PACK - 1):
-            nc.vector.tensor_copy(slot(t, low, high), pieces[t][:])
+            end = high - LEFT_OVER if t == PACK - 2 else high
+            nc.vector.tensor_copy(slot(t, low, end), pieces[t][:, 0 : end - low])
         nc.vector.tensor_copy(pieces[PACK - 1][:], looked_up(planes[PACK - 1], low, high))
+        nc.vector.tensor_copy(slot(PACK - 2, high - LEFT_OVER, high), pieces[PACK - 2][:, high - LEFT_OVER - low :])
         for a, b in LAST_ON_SCALAR:
             nc.scalar.activation(slot(PACK - 1, a, b), looked_up(planes[PACK - 1], a, b), COPY)
 

import concourse.mybir as mybir
from concourse.masks import make_identity

K, T, S, N = 512, 4096, 1024, 128
FLOPS = 2 * K * S * N
BYTES = 4 * (K * T + T + N + K * N + N * S) + 2 * 128 * (S // 16)

F32 = mybir.dt.float32
BF16 = mybir.dt.bfloat16
U32 = mybir.dt.uint32
U16 = mybir.dt.uint16
U8 = mybir.dt.uint8
FP8X4 = mybir.dt.float8_e4m3fn_x4
MULT = mybir.AluOpType.mult
COPY = mybir.ActivationFunctionType.Copy

P = 128
PACK = 4
RUNS = T // P
RUN_STEP = P // RUNS
PER_BANK = 4
BURST = 256
ON_VECTOR = (128, 320)
LAST_ON_SCALAR = ((0, 128), (320, 512), (512, 768), (768, 896), (896, 1024),)
SCALES_ON_SCALAR = ()
SCALES_ON_VECTOR = ((0, 1024),)
PIECE_BYTES = 384
LEFT_OVER = 128
STORES = ((0, 128), (128, 384), (384, 640), (640, 896), (896, 1024),)
TAIL = (
    ("place", 128, 320, None),
    ("weave", 0, 0, None),
    ("quantise", 0, 128, None),
    ("weights", 0, 0, None),
    ("product", 0, 128, None),
    ("quantise", 128, 256, None),
    ("product", 128, 256, None),
    ("quantise", 256, 512, None),
    ("product", 256, 384, None),
    ("product", 384, 512, None),
    ("quantise", 512, 768, None),
    ("product", 512, 640, None),
    ("product", 640, 768, None),
    ("scale", 0, 128, None),
    ("quantise", 768, 896, None),
    ("product", 768, 896, None),
    ("scale", 128, 256, None),
    ("scale", 256, 384, None),
    ("quantise", 896, 1024, None),
    ("product", 896, 1024, None),
    ("scale", 384, 512, None),
    ("scale", 512, 640, None),
    ("scale", 640, 768, None),
    ("scale", 768, 896, None),
    ("scale", 896, 1024, None),
)


def tile_picked_tokscale_none_l_kernel(tc, xT, tscale, cscale, w1, offs, out):
    nc = tc.nc
    with (
        tc.tile_pool(name="keep", bufs=1) as keep,
        tc.tile_pool(name="shared", bufs=1) as shared,
        tc.tile_pool(name="early", bufs=1) as early,
        tc.psum_pool(name="psum", bufs=1) as psum,
    ):
        offsets = keep.tile([P, S // 16], U16, name="offsets", align_bytes=BURST)
        ts_runs = keep.tile([P, P], F32, name="ts_runs", align_bytes=BURST)
        nc.vector.memset(ts_runs[:], 0.0)
        nc.scalar.dma_start(ts_runs[0:P:RUN_STEP, :], tscale[0, :].rearrange("(q c) -> q c", c=P))
        x_rows = xT.rearrange("(p t) c -> t p c", t=PACK)
        planes = [keep.tile([P, T], F32, name=f"plane{t}", align_bytes=BURST) for t in range(PACK)]
        for t in range(PACK):
            nc.sync.dma_start(planes[t][:], x_rows[t])
            if t == 0:
                nc.sync.dma_start(offsets[:], offs)
        w_raw = shared.tile([P, PACK, N], F32, name="w_raw", align_bytes=BURST, offset=0)
        nc.sync.dma_start(w_raw[:], w1.rearrange("(p t) n -> p t n", t=PACK))
        cs = keep.tile([P, 1], F32, name="cs")
        nc.sync.dma_start(cs[:], cscale)

        ident = early.tile([P, P], F32, name="ident", offset=PIECE_BYTES - BURST)
        make_identity(nc, ident[:])
        turned = psum.tile([P, P], F32, name="turned", tag="bank7")
        nc.tensor.transpose(turned[:], ts_runs[:], ident[:])
        ts_cols = early.tile([P, RUNS], F32, name="ts_cols", offset=3 * PIECE_BYTES - 64)
        nc.vector.tensor_copy(ts_cols[:], turned[:, 0:P:RUN_STEP])
        ts_window = keep.tile([P, T], F32, name="ts_window")
        for b in range(RUNS // PER_BANK):
            bank = psum.tile([P, PER_BANK * P], F32, name=f"spread{b}", tag=f"bank{b}")
            for i in range(PER_BANK):
                q = b * PER_BANK + i
                nc.tensor.transpose(bank[:, i * P : (i + 1) * P], ts_cols[:, q : q + 1].to_broadcast([P, P]), ident[:])
            nc.vector.tensor_copy(ts_window[:, b * PER_BANK * P : (b + 1) * PER_BANK * P], bank[:])

        def looked_up(window, a, b):
            return window[:].indirect(offsets[:, a // 16 : b // 16])

        token_scale = []
        for a, b in SCALES_ON_SCALAR + SCALES_ON_VECTOR:
            tile = keep.tile([P, b - a], F32, name=f"scale{a}", tag=f"scale{a}", align_bytes=BURST)
            if (a, b) in SCALES_ON_SCALAR:
                nc.scalar.activation(tile[:], looked_up(ts_window, a, b), COPY)
            else:
                nc.vector.tensor_copy(tile[:], looked_up(ts_window, a, b))
            token_scale.append((a, b, tile))

        def within(tiles, a, b):
            start, tile = [(lo, tile) for lo, hi, tile in tiles if lo <= a and b <= hi][0]
            return tile[:, a - start : b - start]

        grouped = keep.tile([P, S * PACK], BF16, name="grouped", align_bytes=64)

        def slot(t, a, b):
            return grouped[:, a * PACK : b * PACK].rearrange("p (n t) -> p n t", t=PACK)[:, :, t]

        low, high = ON_VECTOR
        pieces = [early.tile([P, high - low], BF16, name=f"piece{t}", offset=t * PIECE_BYTES) for t in range(PACK)]
        for t in range(PACK - 1):
            nc.vector.tensor_copy(pieces[t][:], looked_up(planes[t], low, high))
            for a, b in ((0, low), (high, S)):
                if a < b:
                    nc.scalar.activation(slot(t, a, b), looked_up(planes[t], a, b), COPY)
        for t in range(PACK - 1):
            end = high - LEFT_OVER if t == PACK - 2 else high
            nc.vector.tensor_copy(slot(t, low, end), pieces[t][:, 0 : end - low])
        nc.vector.tensor_copy(pieces[PACK - 1][:], looked_up(planes[PACK - 1], low, high))
        nc.vector.tensor_copy(slot(PACK - 2, high - LEFT_OVER, high), pieces[PACK - 2][:, high - LEFT_OVER - low :])
        for a, b in LAST_ON_SCALAR:
            nc.scalar.activation(slot(PACK - 1, a, b), looked_up(planes[PACK - 1], a, b), COPY)

        w_grouped = keep.tile([P, N, PACK], BF16, name="w_grouped", align_bytes=64)
        w_codes = keep.tile([P, N], U32, name="w_codes", align_bytes=64)
        w_scales = keep.tile([P, N], U8, name="w_scales", align_bytes=64)
        result = keep.tile([P, S], F32, name="result", align_bytes=BURST)
        all_codes = []
        all_scales = []
        products = []
        over_weights = []
        finished = []

        for step, a, b, over in TAIL:
            if step == "weave":
                nc.vector.tensor_copy(
                    w_grouped[:].rearrange("p (c i) t -> p c t i", i=PACK),
                    w_raw[:].rearrange("p t (c i) -> p c t i", i=PACK),
                )
            elif step == "place":
                nc.vector.tensor_copy(slot(PACK - 1, a, b), pieces[PACK - 1][:, a - low : b - low])
            elif step == "weights":
                nc.vector.quantize_mx(
                    out=w_codes[:].bitcast(FP8X4), scales=w_scales[:], in_=w_grouped[:].rearrange("p n t -> p (n t)")
                )
            elif step == "quantise":
                codes = keep.tile([P, b - a], U32, name=f"codes{a}", align_bytes=BURST)
                if over == "weights":
                    at = len(over_weights) * BURST
                    over_weights.append(a)
                    scales = shared.tile([P, b - a], U8, name=f"scales{a}", align_bytes=BURST, offset=at)
                else:
                    scales = keep.tile([P, b - a], U8, name=f"scales{a}", tag=over or f"scales{a}", align_bytes=BURST)
                nc.vector.quantize_mx(out=codes[:].bitcast(FP8X4), scales=scales[:], in_=grouped[:, a * PACK : b * PACK])
                all_codes.append((a, b, codes))
                all_scales.append((a, b, scales))
            elif step == "product":
                acc = psum.tile([P, b - a], F32, name=f"acc{a}", tag=f"bank{len(products) % 8}")
                nc.tensor.matmul_mx(
                    out=acc[:],
                    lhsT=w_codes[:].bitcast(FP8X4),
                    lhsT_scale=w_scales[:],
                    rhs=within(all_codes, a, b).bitcast(FP8X4),
                    rhs_scale=within(all_scales, a, b),
                    start=True,
                    stop=True,
                )
                products.append((a, b, acc))
            else:
                acc, factor = within(products, a, b), within(token_scale, a, b)
                if step == "scale":
                    nc.vector.scalar_tensor_tensor(result[:, a:b], factor, cs[:, 0:1], acc, MULT, MULT)
                else:
                    aside = keep.tile([P, b - a], F32, name=f"aside{a}")
                    nc.scalar.activation(aside[:], acc, COPY, scale=cs[:, 0:1])
                    nc.gpsimd.tensor_tensor(result[:, a:b], aside[:], factor, MULT)
                finished.extend(range(a, b))
                for first, end in STORES:
                    if first < b and a < end and all(j in finished for j in range(first, end)):
                        nc.sync.dma_start(out[:, first:end], result[:, first:end])
